import numpy as np
import ml_dtypes


def mxq(x, axis, fmt="e4m3"):
    dtype, down = {"e4m3": (ml_dtypes.float8_e4m3fn, 7), "e5m2": (ml_dtypes.float8_e5m2, 14)}[fmt]
    v = np.moveaxis(np.asarray(x, np.float32).astype(ml_dtypes.bfloat16).astype(np.float64), axis, -1)
    blocks = v.reshape(v.shape[:-1] + (-1, 32))
    amax = np.abs(blocks).max(-1, keepdims=True)
    byte = np.maximum(np.where(amax > 0, np.frexp(amax)[1] - 1 + 127, 0) - down, 1)
    scale = np.exp2(byte - 127.0)
    codes = (blocks / scale).astype(np.float32).astype(dtype).astype(np.float64)
    return np.moveaxis((codes * scale).reshape(v.shape), -1, axis)


WIDE = False


def mx_kscale(k):
    if not WIDE:
        return np.ones(k)
    levels = np.array([10, -10, 5, -5, 0])
    if k % 512:
        return np.exp2(np.random.permutation(np.resize(levels, k // 32))).repeat(32)
    a = np.empty((k // 512, 16))
    for p in range(k // 512):
        a[p, :8] = np.random.permutation(np.resize(levels, 8))
        for g in range(8):
            far = levels[np.abs(levels - a[p, g]) >= 10]
            a[p, g + 8] = far[np.random.randint(len(far))]
    return np.exp2(a.ravel()).repeat(32)


BF16 = ml_dtypes.bfloat16


def bf(x):
    return np.asarray(x, np.float32).astype(BF16)


def f64(x):
    return np.asarray(x).astype(np.float64)


E2M1 = np.array([0.0, 0.5, 1.0, 1.5, 2.0, 3.0, 4.0, 6.0, -0.0, -0.5, -1.0, -1.5, -2.0, -3.0, -4.0, -6.0])


def pack_weight(w, fmt):
    k, n = w.shape
    w = f64(bf(w)).reshape(k // 32, 32, n)
    amax = np.abs(w).max(1)
    if fmt == "e4m3":
        byte = np.frexp(amax)[1] - 1 + 127 - 7
    else:
        mant, ex = np.frexp(amax / 6.0)
        byte = np.where(mant > 0.5, ex, ex - 1) + 127
    byte = np.clip(np.where(amax > 0, byte, 1), 1, 254)
    scaled = (w * np.exp2(127.0 - byte)[:, None, :]).reshape(k, n).astype(np.float32)
    by_word = np.ascontiguousarray(scaled.reshape(k // 512, 128, 4, n).transpose(0, 1, 3, 2))
    if fmt == "e4m3":
        words = by_word.astype(ml_dtypes.float8_e4m3fn).view(np.uint8)
    else:
        c = by_word.astype(ml_dtypes.float4_e2m1fn).view(np.uint8) & 0xF
        words = c[..., 0::2] | (c[..., 1::2] << 4)
    return np.ascontiguousarray(words), np.ascontiguousarray(byte.astype(np.uint8).reshape(k // 512, 16, n))


def unpack_weight(words, scales, fmt):
    g, p, n, _ = words.shape
    if fmt == "e4m3":
        vals = np.ascontiguousarray(words).view(ml_dtypes.float8_e4m3fn).astype(np.float64)
    else:
        nib = np.empty((g, p, n, 4), np.uint8)
        nib[..., 0::2] = words & 0xF
        nib[..., 1::2] = words >> 4
        vals = E2M1[nib]
    vals = vals * np.repeat(np.exp2(scales.astype(np.float64) - 127.0), 8, axis=1)[..., None]
    return vals.transpose(0, 1, 3, 2).reshape(g * 512, n)
def pack4(w):
    words, scales = pack_weight(w, "e2m1")
    return words.reshape(words.shape[0], 128, -1), scales


def unpack4(words, scales):
    return unpack_weight(words.reshape(words.shape[0], 128, -1, 2), scales, "e2m1")


def planes(Y):
    n, m = Y.shape
    b = f64(bf(Y)).reshape(n // 32, 32, m)
    amax = np.abs(b).max(1)
    byte = np.clip(np.where(amax > 0, np.frexp(amax)[1] - 1 + 127 - 7, 1), 1, 254)
    codes = (b * np.exp2(127.0 - byte)[:, None, :]).reshape(n, m).astype(np.float32).astype(ml_dtypes.float8_e4m3fn).view(np.uint8)
    words = codes.reshape(n // 512, 128, 4, m).transpose(0, 1, 3, 2)
    return np.ascontiguousarray(words), np.ascontiguousarray(byte.astype(np.uint8).reshape(n // 512, 16, m))


G, N, D, R, M, L = 4, 1024, 512, 1024, 512, 8
SHARE = 0.35

def mix(z, b):
    return sum(z[:, :, l, None] * b[:, None, l, :] for l in range(L))

def setup_inputs():
    s, t = mx_kscale(D), mx_kscale(R)
    width2 = D / (SHARE * L)
    b = np.random.randn(G, L, D) / np.sqrt(L)
    x = mix(np.random.randn(G, N, L), b)
    c = mix(np.random.randn(G, R, L), b)
    rowfac = np.exp(-(x ** 2).sum(2) / (2.0 * width2))
    rulefac = np.random.uniform(0.5, 1.0, (G, R)) * np.exp(-(c ** 2).sum(2) / (2.0 * width2))
    C = (c / width2).transpose(0, 2, 1) / s[:, None]
    spread = np.exp(0.8 * np.random.randn(M))
    F = 6.0 * np.random.randn(G, R, M) / np.sqrt(R) * spread / t[:, None]
    c_words, c_scales = pack4(C.reshape(G * D, R))
    f_words, f_scales = pack4(F.reshape(G * R, M))
    return {"x": bf(x * s), "c_words": c_words, "c_scales": c_scales,
            "rulefac": bf(rulefac * t), "f_words": f_words, "f_scales": f_scales,
            "rowfac": bf(rowfac), "err": bf(np.random.randn(G, N, M)),
            "u0": bf(0.3 * np.random.randn(G, M) * spread)}

def reference(x, c_words, c_scales, rulefac, f_words, f_scales, rowfac, err, u0):
    C = unpack4(c_words, c_scales).reshape(G, D, R)
    F = unpack4(f_words, f_scales).reshape(G, R, M)
    S = mxq(f64(x), 2, "e4m3") @ C
    H = np.exp(S) * f64(rulefac)[:, None, :]
    gain = (mxq(H, 2, "e4m3") @ F) * f64(rowfac)[:, :, None]
    y = gain * f64(err) + f64(u0)[:, None, :]
    Y = y.reshape(G * N, M).T
    words, scales = planes(Y)
    return y, words, scales

@@ -1,0 +1,334 @@
+from contextlib import ExitStack
+
+import concourse.mybir as mybir
+from concourse.masks import make_identity
+
+F32 = mybir.dt.float32
+BF16 = mybir.dt.bfloat16
+I32 = mybir.dt.int32
+U32 = mybir.dt.uint32
+U8 = mybir.dt.uint8
+FP8X4 = mybir.dt.float8_e4m3fn_x4
+FP4X4 = mybir.dt.float4_e2m1fn_x4
+ALU = mybir.AluOpType
+ACT = mybir.ActivationFunctionType
+
+G, N, D, R, M = 4, 1024, 512, 1024, 512
+P = 128
+UNIT = 256
+UNITS = G * N // UNIT
+PER_GROUP = N // UNIT
+FLOPS = 2 * G * N * D * R + 2 * G * N * R * M
+
+
+def tile_takagi_sugeno_gain_blend_k7_kernel(
+    tc, x, c_words, c_scales, rulefac, f_words, f_scales, rowfac, err, u0, out_0, out_1, out_2
+):
+    nc = tc.nc
+    x_rows = x.rearrange("g n d -> (g n) d")
+    err_rows = err.rearrange("g n j -> (g n) j")
+    y_rows = out_0.rearrange("g n j -> (g n) j")
+    out_words = out_1[0].rearrange("p m t -> p (m t)").bitcast(I32)
+
+    with ExitStack() as ctx:
+        keep = ctx.enter_context(tc.tile_pool(name="keep", bufs=1))
+        work = ctx.enter_context(tc.tile_pool(name="work", bufs=2))
+        psum = ctx.enter_context(tc.psum_pool(name="psum", bufs=1))
+        ctx.enter_context(tc.manual_schedule())
+
+        t = {}
+
+        def unit_rows(rows, i):
+            return rows[UNIT * i : UNIT * (i + 1), :].rearrange("(p s) c -> p (s c)", s=2)
+
+        def load_x(i):
+            t["x", i] = work.tile([P, 2 * D], BF16, name="x_sb", bufs=4)
+            nc.sync.dma_start(out=t["x", i][:], in_=unit_rows(x_rows, i))
+
+        def load_err(i):
+            t["err", i] = work.tile([P, 2 * M], BF16, name="err_sb", bufs=4)
+            nc.sync.dma_start(out=t["err", i][:], in_=unit_rows(err_rows, i))
+
+        def load_c_words(g):
+            t["c_raw", g] = keep.tile([P, 2 * R], U8, name="c_raw%d" % g)
+            nc.sync.dma_start(out=t["c_raw", g][:].bitcast(I32), in_=c_words[g].bitcast(I32))
+
+        def load_scale_rows(plane, rows):
+            count = rows.shape[0]
+            for q in range(4):
+                nc.sync.dma_start(
+                    out=plane[32 * q : 32 * q + 4, :].bitcast(I32).rearrange("r (c n) -> r c n", c=count),
+                    in_=rows[:, 4 * q : 4 * q + 4, :].rearrange("c r n -> r c n").bitcast(I32),
+                )
+
+        def load_group(g):
+            t["f_words", g] = keep.tile([P, 4 * M], U8, name="f_words%d" % g, align_bytes=64)
+            nc.sync.dma_start(
+                out=t["f_words", g][:].bitcast(I32).rearrange("p (c n) -> p c n", c=2),
+                in_=f_words[2 * g : 2 * g + 2].rearrange("c p n -> p c n").bitcast(I32),
+            )
+
+        def load_u0(g):
+            t["u0", g] = keep.tile([P, M], BF16, name="u0_%d" % g)
+            nc.sync.dma_start(out=t["u0", g][:], in_=u0[g].partition_broadcast(P))
+
+        def sort_c_words(g, h):
+            if h == 0:
+                t["c", g] = keep.tile([P, 2 * R], U8, name="c_sorted%d" % g, align_bytes=64)
+            cols = slice(1024 * h, 1024 * (h + 1))
+            nc.vector.tensor_copy(
+                out=t["c", g][:, cols].rearrange("p (t m b) -> p t m b", t=4, b=2),
+                in_=t["c_raw", g][:, cols].rearrange("p (m t b) -> p t m b", t=4, b=2),
+            )
+
+        def sort_c_scales(g):
+            t["cs", g] = keep.tile([P, R], U8, name="cs_sorted%d" % g, align_bytes=64)
+            nc.vector.tensor_copy(
+                out=t["cs", g][:].rearrange("p (h t m) -> p h t m", h=2, t=4),
+                in_=t["cs_raw", g].rearrange("p (h m t) -> p h t m", h=2, t=4),
+            )
+
+        def turn(src, bank):
+            words = src[:].bitcast(F32)
+            for s in range(2):
+                for u in range(2):
+                    nc.tensor.transpose(
+                        bank[:, P * (2 * s + u) : P * (2 * s + u + 1)],
+                        words[:, 256 * s + u : 256 * (s + 1) : 2],
+                        ident[:],
+                    )
+
+        def turn_x(i):
+            t["xT", i] = psum.tile([P, 512], F32, name="x_bank")
+            turn(t["x", i], t["xT", i])
+
+        def copy_x(i):
+            t["xb", i] = work.tile([P, 4 * UNIT], BF16, name="x_grouped", align_bytes=64)
+            nc.scalar.copy(
+                out=t["xb", i][:].bitcast(F32).rearrange("k (s p u) -> k s p u", s=2, u=2),
+                in_=t["xT", i][:].rearrange("k (s u p) -> k s p u", s=2, u=2),
+            )
+
+        def quantize_x(i):
+            t["xq", i] = work.tile([P, UNIT], U32, name="x_codes", bufs=3, align_bytes=64)
+            t["xs", i] = work.tile([P, UNIT], U8, name="x_scales", bufs=3, align_bytes=64)
+            nc.vector.quantize_mx(out=t["xq", i][:].bitcast(FP8X4), scales=t["xs", i][:], in_=t["xb", i][:])
+
+        def first_product(i, b):
+            g = i // PER_GROUP
+            t["S", i, b] = psum.tile([P, 512], F32, name="s_bank", bufs=3)
+            for e in range(2):
+                col = 2 * b + e
+                nc.tensor.matmul_mx(
+                    out=t["S", i, b][:, UNIT * e : UNIT * (e + 1)],
+                    lhsT=t["c", g][:, 2 * P * col : 2 * P * (col + 1)].bitcast(FP4X4),
+                    lhsT_scale=t["cs", g][:, P * col : P * (col + 1)],
+                    rhs=t["xq", i][:].bitcast(FP8X4),
+                    rhs_scale=t["xs", i][:],
+                    start=True,
+                    stop=True,
+                )
+
+        def exponential(i, b):
+            h, u = divmod(b, 2)
+            if u == 0:
+                t["E", i, h] = work.tile([P, 1024], F32, name="exp_s", bufs=4)
+            nc.scalar.activation(
+                out=t["E", i, h][:, 512 * u : 512 * (u + 1)].rearrange("p (n e) -> p n e", e=2),
+                in_=t["S", i, b][:].rearrange("p (e n) -> p n e", e=2),
+                func=ACT.Exp,
+            )
+
+        def times_rulefac(i, h):
+            row = 2 * (i // PER_GROUP) + h
+            if h == 0:
+                t["H", i] = work.tile([P, 8 * UNIT], BF16, name="h_grouped", align_bytes=64)
+            nc.vector.tensor_tensor(
+                out=t["H", i][:, 1024 * h : 1024 * (h + 1)].rearrange("p (n u e) -> p n u e", u=2, e=2),
+                in0=t["E", i, h][:].rearrange("p (u n e) -> p n u e", u=2, e=2),
+                in1=rule_pairs[:, :, 2 * row : 2 * row + 2].unsqueeze(1).to_broadcast([P, UNIT, 2, 2]),
+                op=ALU.mult,
+            )
+
+        def quantize_h(i):
+            t["hq", i] = work.tile([P, 2 * UNIT], U32, name="h_codes", bufs=3, align_bytes=64)
+            t["hs", i] = work.tile([P, 2 * UNIT], U8, name="h_scales", bufs=3, align_bytes=64)
+            nc.vector.quantize_mx(out=t["hq", i][:].bitcast(FP8X4), scales=t["hs", i][:], in_=t["H", i][:])
+
+        def second_product(i):
+            g = i // PER_GROUP
+            for s in range(2):
+                t["U", i, s] = psum.tile([P, M], F32, name="u_bank", bufs=2)
+                for h in range(2):
+                    cols = slice(UNIT * h + P * s, UNIT * h + P * (s + 1))
+                    nc.tensor.matmul_mx(
+                        out=t["U", i, s][:],
+                        lhsT=t["hq", i][:, cols].bitcast(FP8X4),
+                        lhsT_scale=t["hs", i][:, cols],
+                        rhs=t["f_words", g][:, 2 * M * h : 2 * M * (h + 1)].bitcast(FP4X4),
+                        rhs_scale=f_plane[:, M * (2 * g + h) : M * (2 * g + h + 1)],
+                        start=(h == 0),
+                        stop=(h == 1),
+                    )
+
+        def times_err(i):
+            for s in range(2):
+                t["V", i, s] = work.tile([P, M], F32, name="gain_err", bufs=4)
+                nc.vector.scalar_tensor_tensor(
+                    out=t["V", i, s][:],
+                    in0=t["U", i, s][:],
+                    scalar=row_f32[:, 2 * i + s : 2 * i + s + 1],
+                    in1=t["err", i][:, M * s : M * (s + 1)],
+                    op0=ALU.mult,
+                    op1=ALU.mult,
+                )
+
+        def add_u0(i):
+            t["y", i] = work.tile([P, 2 * M], F32, name="y_sb", bufs=4)
+            for s in range(2):
+                nc.gpsimd.tensor_tensor(
+                    out=t["y", i][:, M * s : M * (s + 1)],
+                    in0=t["V", i, s][:],
+                    in1=t["u0", i // PER_GROUP][:],
+                    op=ALU.add,
+                )
+            nc.sync.dma_start(out=unit_rows(y_rows, i), in_=t["y", i][:])
+
+        def round_y(i):
+            t["yb", i] = work.tile([P, 2 * M], BF16, name="y_bf16")
+            nc.scalar.copy(out=t["yb", i][:], in_=t["y", i][:])
+
+        def turn_y(i):
+            t["yT", i] = psum.tile([P, 512], F32, name="y_bank")
+            turn(t["yb", i], t["yT", i])
+
+        def copy_y(i):
+            t["yg", i] = work.tile([P, 4 * UNIT], BF16, name="y_grouped", align_bytes=64)
+            nc.scalar.copy(
+                out=t["yg", i][:].bitcast(F32).rearrange("k (p s u) -> k p s u", s=2, u=2),
+                in_=t["yT", i][:].rearrange("k (s u p) -> k p s u", s=2, u=2),
+            )
+
+        def quantize_y(i):
+            g, j = divmod(i, PER_GROUP)
+            if i % 2 == 0:
+                t["yq", i // 2] = work.tile([P, 2 * UNIT], U32, name="y_codes", bufs=3, align_bytes=64)
+            if j == 0:
+                t["ys", g] = work.tile([P, N], U8, name="y_scales", align_bytes=64)
+            codes = t["yq", i // 2]
+            nc.vector.quantize_mx(
+                out=codes[:, UNIT * (i % 2) : UNIT * (i % 2 + 1)].bitcast(FP8X4),
+                scales=t["ys", g][:, UNIT * j : UNIT * (j + 1)],
+                in_=t["yg", i][:],
+            )
+            if i % 2 == 1:
+                nc.sync.dma_start(out=out_words[:, UNIT * (i - 1) : UNIT * (i + 1)], in_=codes[:].bitcast(I32))
+            if j == PER_GROUP - 1:
+                for q in range(4):
+                    nc.sync.dma_start(
+                        out=out_2[0, 4 * q : 4 * q + 4, N * g : N * (g + 1)].bitcast(I32),
+                        in_=t["ys", g][32 * q : 32 * q + 4, :].bitcast(I32),
+                    )
+
+        ident = keep.tile([P, P], F32)
+        cs_first = keep.tile([P, R], U8)
+        cs_rest = keep.tile([P, (G - 1) * R], U8)
+        f_plane = keep.tile([P, 2 * G * M], U8, align_bytes=64)
+        rule_rows = keep.tile([P, 512], BF16)
+        row_bf16 = keep.tile([P, 2 * UNITS], BF16)
+        row_f32 = keep.tile([P, 2 * UNITS], F32)
+        warm = keep.tile([P, 2], F32)
+
+        nc.vector.memset(cs_first[:].bitcast(I32), 0)
+        nc.vector.memset(warm[:], 0.0)
+        nc.scalar.activation(out=warm[:, 1:2], in_=warm[:, 0:1], func=ACT.Exp)
+        nc.vector.memset(rule_rows[:], 0.0)
+        make_identity(nc, ident[:])
+        nc.vector.memset(cs_rest[:].bitcast(I32), 0)
+        nc.vector.memset(f_plane[:].bitcast(I32), 0)
+
+        t["cs_raw", 0] = cs_first[:]
+        for g in range(1, G):
+            t["cs_raw", g] = cs_rest[:, R * (g - 1) : R * g]
+
+        load_x(0)
+        load_c_words(0)
+        load_scale_rows(cs_first, c_scales[0:1])
+        nc.sync.dma_start(out=rule_rows[0 : 2 * G, :], in_=rulefac.rearrange("g (h r) -> (g h) r", h=2))
+        load_x(1)
+        load_c_words(1)
+        load_x(2)
+        load_scale_rows(cs_rest, c_scales[1:G])
+        load_group(0)
+        load_scale_rows(f_plane, f_scales)
+        nc.sync.dma_start(
+            out=row_bf16[:].rearrange("p (i s) -> p i s", s=2),
+            in_=rowfac.rearrange("g (j p s) -> p (g j) s", p=P, s=2),
+        )
+        load_u0(0)
+
+        turn_x(0)
+        rule_bank = psum.tile([P, 512], F32)
+        rule_words = rule_rows[:].bitcast(F32)
+        for u in range(2):
+            nc.tensor.transpose(rule_bank[:, P * u : P * (u + 1)], rule_words[:, u : 256 : 2], ident[:])
+        rule_pairs = rule_bank[:, 0 : 2 * P].bitcast(BF16).rearrange("p (u c) -> p u c", u=2)
+        nc.gpsimd.tensor_copy(out=row_f32[:], in_=row_bf16[:])
+        sort_c_words(0, 0)
+        sort_c_scales(0)
+        sort_c_words(0, 1)
+
+        def live(i):
+            return 0 <= i < UNITS
+
+        sort_at = {-2: (1, 0), -1: (1, 1), 0: (1, 2), 3: (2, 0), 4: (2, 1), 5: (2, 2), 7: (3, 0), 8: (3, 1), 9: (3, 2)}
+
+        for s in range(-2, UNITS + 4):
+            if live(s + 5):
+                load_x(s + 5)
+            if live(s + 1):
+                load_err(s + 1)
+            if s in (0, 4):
+                load_c_words(s // 4 + 2)
+            if s in (1, 5, 9):
+                load_group(s // 4 + 1)
+                load_u0(s // 4 + 1)
+            if live(s - 2):
+                times_err(s - 2)
+                add_u0(s - 2)
+            if live(s + 2):
+                copy_x(s + 2)
+            if live(s + 1):
+                for b in range(3):
+                    first_product(s + 1, b)
+            if live(s - 3):
+                round_y(s - 3)
+            if live(s - 1):
+                second_product(s - 1)
+            if live(s):
+                times_rulefac(s, 0)
+                times_rulefac(s, 1)
+            if live(s + 1):
+                exponential(s + 1, 0)
+                first_product(s + 1, 3)
+            if live(s - 4):
+                copy_y(s - 4)
+            if live(s + 3):
+                turn_x(s + 3)
+            if live(s - 3):
+                turn_y(s - 3)
+            if live(s + 1):
+                for b in range(1, 4):
+                    exponential(s + 1, b)
+            if live(s - 4):
+                quantize_y(s - 4)
+            if live(s + 2):
+                quantize_x(s + 2)
+            if s in sort_at:
+                g, piece = sort_at[s]
+                if piece < 2:
+                    sort_c_words(g, piece)
+                else:
+                    sort_c_scales(g)
+            if live(s):
+                quantize_h(s)

@@ -81,12 +81,18 @@ def tile_takagi_sugeno_gain_blend_k7_kernel(
                 in_=t["c_raw", g][:, cols].rearrange("p (m t b) -> p t m b", t=4, b=2),
             )
 
-        def sort_c_scales(g):
-            t["cs", g] = keep.tile([P, R], U8, name="cs_sorted%d" % g, align_bytes=64)
+        def sort_c_scales():
             nc.vector.tensor_copy(
-                out=t["cs", g][:].rearrange("p (h t m) -> p h t m", h=2, t=4),
-                in_=t["cs_raw", g].rearrange("p (h m t) -> p h t m", h=2, t=4),
+                out=t["cs", 0].rearrange("p (h t m) -> p h t m", h=2, t=4),
+                in_=cs_packed[:].rearrange("p (h m t) -> p h t m", h=2, t=4),
             )
+
+        def spread_c_scales(g):
+            for q in range(4):
+                nc.sync.dma_start(
+                    out=t["cs", g][32 * q : 32 * q + 4, :].bitcast(I32),
+                    in_=t["cs", 0][32 * q + 4 * g : 32 * q + 4 * g + 4, :].bitcast(I32),
+                )
 
         def turn(src, bank):
             words = src[:].bitcast(F32)
@@ -155,21 +161,20 @@ def tile_takagi_sugeno_gain_blend_k7_kernel(
             t["hs", i] = work.tile([P, 2 * UNIT], U8, name="h_scales", bufs=3, align_bytes=64)
             nc.vector.quantize_mx(out=t["hq", i][:].bitcast(FP8X4), scales=t["hs", i][:], in_=t["H", i][:])
 
-        def second_product(i):
+        def second_product(i, s):
             g = i // PER_GROUP
-            for s in range(2):
-                t["U", i, s] = psum.tile([P, M], F32, name="u_bank", bufs=2)
-                for h in range(2):
-                    cols = slice(UNIT * h + P * s, UNIT * h + P * (s + 1))
-                    nc.tensor.matmul_mx(
-                        out=t["U", i, s][:],
-                        lhsT=t["hq", i][:, cols].bitcast(FP8X4),
-                        lhsT_scale=t["hs", i][:, cols],
-                        rhs=t["f_words", g][:, 2 * M * h : 2 * M * (h + 1)].bitcast(FP4X4),
-                        rhs_scale=f_plane[:, M * (2 * g + h) : M * (2 * g + h + 1)],
-                        start=(h == 0),
-                        stop=(h == 1),
-                    )
+            t["U", i, s] = psum.tile([P, M], F32, name="u_bank", bufs=2)
+            for h in range(2):
+                cols = slice(UNIT * h + P * s, UNIT * h + P * (s + 1))
+                nc.tensor.matmul_mx(
+                    out=t["U", i, s][:],
+                    lhsT=t["hq", i][:, cols].bitcast(FP8X4),
+                    lhsT_scale=t["hs", i][:, cols],
+                    rhs=t["f_words", g][:, 2 * M * h : 2 * M * (h + 1)].bitcast(FP4X4),
+                    rhs_scale=f_plane[:, M * (2 * g + h) : M * (2 * g + h + 1)],
+                    start=(h == 0),
+                    stop=(h == 1),
+                )
 
         def times_err(i):
             for s in range(2):
@@ -184,19 +189,29 @@ def tile_takagi_sugeno_gain_blend_k7_kernel(
                 )
 
         def add_u0(i):
+            last = i == UNITS - 1
             t["y", i] = work.tile([P, 2 * M], F32, name="y_sb", bufs=4)
             for s in range(2):
-                nc.gpsimd.tensor_tensor(
+                (nc.vector if last else nc.gpsimd).tensor_tensor(
                     out=t["y", i][:, M * s : M * (s + 1)],
                     in0=t["V", i, s][:],
                     in1=t["u0", i // PER_GROUP][:],
                     op=ALU.add,
                 )
-            nc.sync.dma_start(out=unit_rows(y_rows, i), in_=t["y", i][:])
+                if last:
+                    nc.sync.dma_start(
+                        out=unit_rows(y_rows, i)[:, M * s : M * (s + 1)], in_=t["y", i][:, M * s : M * (s + 1)]
+                    )
+            if not last:
+                nc.sync.dma_start(out=unit_rows(y_rows, i), in_=t["y", i][:])
 
         def round_y(i):
             t["yb", i] = work.tile([P, 2 * M], BF16, name="y_bf16")
-            nc.scalar.copy(out=t["yb", i][:], in_=t["y", i][:])
+            parts = 2 if i == UNITS - 1 else 1
+            width = 2 * M // parts
+            for s in range(parts):
+                cols = slice(width * s, width * (s + 1))
+                nc.scalar.copy(out=t["yb", i][:, cols], in_=t["y", i][:, cols])
 
         def turn_y(i):
             t["yT", i] = psum.tile([P, 512], F32, name="y_bank")
@@ -221,25 +236,31 @@ def tile_takagi_sugeno_gain_blend_k7_kernel(
                 scales=t["ys", g][:, UNIT * j : UNIT * (j + 1)],
                 in_=t["yg", i][:],
             )
-            if i % 2 == 1:
+            if i >= UNITS - 2:
+                nc.sync.dma_start(
+                    out=out_words[:, UNIT * i : UNIT * (i + 1)],
+                    in_=codes[:, UNIT * (i % 2) : UNIT * (i % 2 + 1)].bitcast(I32),
+                )
+            elif i % 2 == 1:
                 nc.sync.dma_start(out=out_words[:, UNIT * (i - 1) : UNIT * (i + 1)], in_=codes[:].bitcast(I32))
             if j == PER_GROUP - 1:
                 for q in range(4):
-                    nc.sync.dma_start(
+                    (nc.scalar if g == G - 1 and q % 2 else nc.sync).dma_start(
                         out=out_2[0, 4 * q : 4 * q + 4, N * g : N * (g + 1)].bitcast(I32),
                         in_=t["ys", g][32 * q : 32 * q + 4, :].bitcast(I32),
                     )
 
         ident = keep.tile([P, P], F32)
-        cs_first = keep.tile([P, R], U8)
-        cs_rest = keep.tile([P, (G - 1) * R], U8)
+        cs_packed = keep.tile([P, R], U8)
+        cs_first = keep.tile([P, R], U8, align_bytes=64)
+        cs_rest = keep.tile([P, (G - 1) * R], U8, align_bytes=64)
         f_plane = keep.tile([P, 2 * G * M], U8, align_bytes=64)
         rule_rows = keep.tile([P, 512], BF16)
         row_bf16 = keep.tile([P, 2 * UNITS], BF16)
         row_f32 = keep.tile([P, 2 * UNITS], F32)
         warm = keep.tile([P, 2], F32)
 
-        nc.vector.memset(cs_first[:].bitcast(I32), 0)
+        nc.vector.memset(cs_packed[:].bitcast(I32), 0)
         nc.vector.memset(warm[:], 0.0)
         nc.scalar.activation(out=warm[:, 1:2], in_=warm[:, 0:1], func=ACT.Exp)
         nc.vector.memset(rule_rows[:], 0.0)
@@ -247,18 +268,21 @@ def tile_takagi_sugeno_gain_blend_k7_kernel(
         nc.vector.memset(cs_rest[:].bitcast(I32), 0)
         nc.vector.memset(f_plane[:].bitcast(I32), 0)
 
-        t["cs_raw", 0] = cs_first[:]
+        t["cs", 0] = cs_first[:]
         for g in range(1, G):
-            t["cs_raw", g] = cs_rest[:, R * (g - 1) : R * g]
+            t["cs", g] = cs_rest[:, R * (g - 1) : R * g]
 
         load_x(0)
         load_c_words(0)
-        load_scale_rows(cs_first, c_scales[0:1])
+        for q in range(4):
+            nc.sync.dma_start(
+                out=cs_packed[32 * q : 32 * q + 4 * G, :].bitcast(I32),
+                in_=c_scales[:, 4 * q : 4 * q + 4, :].bitcast(I32),
+            )
         nc.sync.dma_start(out=rule_rows[0 : 2 * G, :], in_=rulefac.rearrange("g (h r) -> (g h) r", h=2))
         load_x(1)
         load_c_words(1)
         load_x(2)
-        load_scale_rows(cs_rest, c_scales[1:G])
         load_group(0)
         load_scale_rows(f_plane, f_scales)
         nc.sync.dma_start(
@@ -275,15 +299,23 @@ def tile_takagi_sugeno_gain_blend_k7_kernel(
         rule_pairs = rule_bank[:, 0 : 2 * P].bitcast(BF16).rearrange("p (u c) -> p u c", u=2)
         nc.gpsimd.tensor_copy(out=row_f32[:], in_=row_bf16[:])
         sort_c_words(0, 0)
-        sort_c_scales(0)
+        sort_c_scales()
         sort_c_words(0, 1)
 
         def live(i):
             return 0 <= i < UNITS
 
-        sort_at = {-2: (1, 0), -1: (1, 1), 0: (1, 2), 3: (2, 0), 4: (2, 1), 5: (2, 2), 7: (3, 0), 8: (3, 1), 9: (3, 2)}
+        sort_at = {-2: (1, 0), -1: (1, 1), 3: (2, 0), 4: (2, 1), 7: (3, 0), 8: (3, 1)}
 
-        for s in range(-2, UNITS + 4):
+        def fill(n):
+            if 0 <= n < 4 * UNITS:
+                first_product(n // 4, n % 4)
+
+        def drain(n):
+            if 0 <= n < 4 * UNITS:
+                exponential(n // 4, n % 4)
+
+        for s in range(-2, UNITS + 3):
             if live(s + 5):
                 load_x(s + 5)
             if live(s + 1):
@@ -293,42 +325,40 @@ def tile_takagi_sugeno_gain_blend_k7_kernel(
             if s in (1, 5, 9):
                 load_group(s // 4 + 1)
                 load_u0(s // 4 + 1)
+            if s in (0, 3, 6):
+                spread_c_scales(s // 3 + 1)
             if live(s - 2):
                 times_err(s - 2)
                 add_u0(s - 2)
-            if live(s + 2):
-                copy_x(s + 2)
-            if live(s + 1):
-                for b in range(3):
-                    first_product(s + 1, b)
+            drain(4 * s + 3)
+            fill(4 * s + 6)
+            if live(s - 1):
+                second_product(s - 1, 0)
             if live(s - 3):
                 round_y(s - 3)
-            if live(s - 1):
-                second_product(s - 1)
+                turn_y(s - 3)
             if live(s):
                 times_rulefac(s, 0)
                 times_rulefac(s, 1)
-            if live(s + 1):
-                exponential(s + 1, 0)
-                first_product(s + 1, 3)
-            if live(s - 4):
-                copy_y(s - 4)
+            drain(4 * s + 4)
+            fill(4 * s + 7)
+            if live(s - 1):
+                second_product(s - 1, 1)
+            if live(s + 2):
+                copy_x(s + 2)
             if live(s + 3):
                 turn_x(s + 3)
+            drain(4 * s + 5)
             if live(s - 3):
-                turn_y(s - 3)
-            if live(s + 1):
-                for b in range(1, 4):
-                    exponential(s + 1, b)
-            if live(s - 4):
-                quantize_y(s - 4)
+                copy_y(s - 3)
             if live(s + 2):
                 quantize_x(s + 2)
             if s in sort_at:
-                g, piece = sort_at[s]
-                if piece < 2:
-                    sort_c_words(g, piece)
-                else:
-                    sort_c_scales(g)
+                sort_c_words(*sort_at[s])
             if live(s):
                 quantize_h(s)
+            if live(s - 3):
+                quantize_y(s - 3)
+            fill(4 * s + 8)
+            drain(4 * s + 6)
+            fill(4 * s + 9)

@@ -122,26 +122,27 @@ def tile_takagi_sugeno_gain_blend_k7_kernel(
 
         def first_product(i, b):
             g = i // PER_GROUP
+            h, s = divmod(b, 2)
             t["S", i, b] = psum.tile([P, 512], F32, name="s_bank", bufs=3)
-            for e in range(2):
-                col = 2 * b + e
+            for slot in range(4):
+                col = 4 * h + slot
                 nc.tensor.matmul_mx(
-                    out=t["S", i, b][:, UNIT * e : UNIT * (e + 1)],
+                    out=t["S", i, b][:, P * slot : P * (slot + 1)],
                     lhsT=t["c", g][:, 2 * P * col : 2 * P * (col + 1)].bitcast(FP4X4),
                     lhsT_scale=t["cs", g][:, P * col : P * (col + 1)],
-                    rhs=t["xq", i][:].bitcast(FP8X4),
-                    rhs_scale=t["xs", i][:],
+                    rhs=t["xq", i][:, P * s : P * (s + 1)].bitcast(FP8X4),
+                    rhs_scale=t["xs", i][:, P * s : P * (s + 1)],
                     start=True,
                     stop=True,
                 )
 
         def exponential(i, b):
-            h, u = divmod(b, 2)
-            if u == 0:
+            h, s = divmod(b, 2)
+            if s == 0:
                 t["E", i, h] = work.tile([P, 1024], F32, name="exp_s", bufs=4)
             nc.scalar.activation(
-                out=t["E", i, h][:, 512 * u : 512 * (u + 1)].rearrange("p (n e) -> p n e", e=2),
-                in_=t["S", i, b][:].rearrange("p (e n) -> p n e", e=2),
+                out=t["E", i, h][:, 512 * s : 512 * (s + 1)].rearrange("p (n t) -> p n t", t=4),
+                in_=t["S", i, b][:].rearrange("p (t n) -> p n t", t=4),
                 func=ACT.Exp,
             )
 
@@ -150,9 +151,9 @@ def tile_takagi_sugeno_gain_blend_k7_kernel(
             if h == 0:
                 t["H", i] = work.tile([P, 8 * UNIT], BF16, name="h_grouped", align_bytes=64)
             nc.vector.tensor_tensor(
-                out=t["H", i][:, 1024 * h : 1024 * (h + 1)].rearrange("p (n u e) -> p n u e", u=2, e=2),
-                in0=t["E", i, h][:].rearrange("p (u n e) -> p n u e", u=2, e=2),
-                in1=rule_pairs[:, :, 2 * row : 2 * row + 2].unsqueeze(1).to_broadcast([P, UNIT, 2, 2]),
+                out=t["H", i][:, 1024 * h : 1024 * (h + 1)].rearrange("p (n t) -> p n t", t=4),
+                in0=t["E", i, h][:].rearrange("p (n t) -> p n t", t=4),
+                in1=rule_quads[:, 4 * row : 4 * row + 4].unsqueeze(1).to_broadcast([P, UNIT, 4]),
                 op=ALU.mult,
             )
 
@@ -176,45 +177,36 @@ def tile_takagi_sugeno_gain_blend_k7_kernel(
                     stop=(h == 1),
                 )
 
-        def times_err(i):
-            for s in range(2):
-                t["V", i, s] = work.tile([P, M], F32, name="gain_err", bufs=4)
-                nc.vector.scalar_tensor_tensor(
-                    out=t["V", i, s][:],
-                    in0=t["U", i, s][:],
-                    scalar=row_f32[:, 2 * i + s : 2 * i + s + 1],
-                    in1=t["err", i][:, M * s : M * (s + 1)],
-                    op0=ALU.mult,
-                    op1=ALU.mult,
-                )
+        def times_err(i, s):
+            t["V", i, s] = work.tile([P, M], F32, name="gain_err", bufs=4)
+            nc.vector.scalar_tensor_tensor(
+                out=t["V", i, s][:],
+                in0=t["err", i][:, M * s : M * (s + 1)],
+                scalar=row_f32[:, 2 * i + s : 2 * i + s + 1],
+                in1=t["U", i, s][:],
+                op0=ALU.mult,
+                op1=ALU.mult,
+            )
 
-        def add_u0(i):
-            last = i == UNITS - 1
-            t["y", i] = work.tile([P, 2 * M], F32, name="y_sb", bufs=4)
-            for s in range(2):
-                (nc.vector if last else nc.gpsimd).tensor_tensor(
-                    out=t["y", i][:, M * s : M * (s + 1)],
-                    in0=t["V", i, s][:],
-                    in1=t["u0", i // PER_GROUP][:],
-                    op=ALU.add,
-                )
-                if last:
-                    nc.sync.dma_start(
-                        out=unit_rows(y_rows, i)[:, M * s : M * (s + 1)], in_=t["y", i][:, M * s : M * (s + 1)]
-                    )
-            if not last:
-                nc.sync.dma_start(out=unit_rows(y_rows, i), in_=t["y", i][:])
+        def add_u0(engine, i, s):
+            if s == 0:
+                t["y", i] = work.tile([P, 2 * M], F32, name="y_sb", bufs=4)
+                t["yb", i] = work.tile([P, 2 * M], BF16, name="y_bf16", bufs=3)
+            engine.tensor_tensor(
+                out=t["y", i][:, M * s : M * (s + 1)],
+                in0=t["V", i, s][:],
+                in1=t["u0", i // PER_GROUP][:],
+                op=ALU.add,
+            )
 
-        def round_y(i):
-            t["yb", i] = work.tile([P, 2 * M], BF16, name="y_bf16")
-            parts = 2 if i == UNITS - 1 else 1
-            width = 2 * M // parts
-            for s in range(parts):
-                cols = slice(width * s, width * (s + 1))
-                nc.scalar.copy(out=t["yb", i][:, cols], in_=t["y", i][:, cols])
+        def store_y(i, cols):
+            nc.sync.dma_start(out=unit_rows(y_rows, i)[:, cols], in_=t["y", i][:, cols])
 
-        def turn_y(i):
-            t["yT", i] = psum.tile([P, 512], F32, name="y_bank")
+        def round_y(copy, i, cols):
+            copy(out=t["yb", i][:, cols], in_=t["y", i][:, cols])
+
+        def turn_y(i, bank_name):
+            t["yT", i] = psum.tile([P, 512], F32, name=bank_name)
             turn(t["yb", i], t["yT", i])
 
         def copy_y(i):
@@ -295,8 +287,8 @@ def tile_takagi_sugeno_gain_blend_k7_kernel(
         rule_bank = psum.tile([P, 512], F32)
         rule_words = rule_rows[:].bitcast(F32)
         for u in range(2):
-            nc.tensor.transpose(rule_bank[:, P * u : P * (u + 1)], rule_words[:, u : 256 : 2], ident[:])
-        rule_pairs = rule_bank[:, 0 : 2 * P].bitcast(BF16).rearrange("p (u c) -> p u c", u=2)
+            nc.tensor.transpose(rule_bank[:, u : 2 * P : 2], rule_words[:, u : 256 : 2], ident[:])
+        rule_quads = rule_bank[:].bitcast(BF16)
         nc.gpsimd.tensor_copy(out=row_f32[:], in_=row_bf16[:])
         sort_c_words(0, 0)
         sort_c_scales()
@@ -315,7 +307,10 @@ def tile_takagi_sugeno_gain_blend_k7_kernel(
             if 0 <= n < 4 * UNITS:
                 exponential(n // 4, n % 4)
 
-        for s in range(-2, UNITS + 3):
+        whole = slice(0, 2 * M)
+        half = [slice(0, M), slice(M, 2 * M)]
+
+        for s in range(-2, UNITS):
             if live(s + 5):
                 load_x(s + 5)
             if live(s + 1):
@@ -328,26 +323,28 @@ def tile_takagi_sugeno_gain_blend_k7_kernel(
             if s in (0, 3, 6):
                 spread_c_scales(s // 3 + 1)
             if live(s - 2):
-                times_err(s - 2)
-                add_u0(s - 2)
-            drain(4 * s + 3)
-            fill(4 * s + 6)
+                for r in range(2):
+                    times_err(s - 2, r)
+                for r in range(2):
+                    add_u0(nc.gpsimd, s - 2, r)
+                store_y(s - 2, whole)
+            if live(s - 3):
+                round_y(nc.scalar.copy, s - 3, whole)
+            if live(s + 2):
+                copy_x(s + 2)
             if live(s - 1):
                 second_product(s - 1, 0)
             if live(s - 3):
-                round_y(s - 3)
-                turn_y(s - 3)
+                turn_y(s - 3, "y_bank")
+            if live(s + 3):
+                turn_x(s + 3)
+            if live(s - 1):
+                second_product(s - 1, 1)
             if live(s):
                 times_rulefac(s, 0)
                 times_rulefac(s, 1)
             drain(4 * s + 4)
             fill(4 * s + 7)
-            if live(s - 1):
-                second_product(s - 1, 1)
-            if live(s + 2):
-                copy_x(s + 2)
-            if live(s + 3):
-                turn_x(s + 3)
             drain(4 * s + 5)
             if live(s - 3):
                 copy_y(s - 3)
@@ -362,3 +359,30 @@ def tile_takagi_sugeno_gain_blend_k7_kernel(
             fill(4 * s + 8)
             drain(4 * s + 6)
             fill(4 * s + 9)
+            drain(4 * s + 7)
+            fill(4 * s + 10)
+
+        a, b, c = UNITS - 3, UNITS - 2, UNITS - 1
+        times_err(b, 0)
+        times_err(b, 1)
+        add_u0(nc.gpsimd, b, 0)
+        store_y(b, half[0])
+        round_y(nc.scalar.copy, a, whole)
+        second_product(c, 0)
+        second_product(c, 1)
+        turn_y(a, "y_bank")
+        times_err(c, 0)
+        times_err(c, 1)
+        copy_y(a)
+        for i, r in ((b, 1), (c, 0), (c, 1)):
+            add_u0(nc.vector, i, r)
+            store_y(i, half[r])
+        for i, r in ((b, 0), (b, 1), (c, 0)):
+            round_y(nc.scalar.copy, i, half[r])
+        turn_y(b, "y_bank")
+        quantize_y(a)
+        round_y(nc.vector.tensor_copy, c, half[1])
+        turn_y(c, "x_bank")
+        for i in (b, c):
+            copy_y(i)
+            quantize_y(i)

@@ -15,9 +15,20 @@ ACT = mybir.ActivationFunctionType
 
 G, N, D, R, M = 4, 1024, 512, 1024, 512
 P = 128
-UNIT = 256
+PACK = 4
+K_PASS = P * PACK
+BANK = 512
+FP4_WORD = 2
+QUADRANTS = 4
+HALVES = 2
+UNIT = P * HALVES
 UNITS = G * N // UNIT
 PER_GROUP = N // UNIT
+RULE_PASSES = R // K_PASS
+S_TILES = RULE_PASSES * HALVES
+S_BANKS = 3
+U_BANKS = 2
+X_AHEAD = 5
 FLOPS = 2 * G * N * D * R + 2 * G * N * R * M
 
 
@@ -36,353 +47,369 @@ def tile_takagi_sugeno_gain_blend_k7_kernel(
         psum = ctx.enter_context(tc.psum_pool(name="psum", bufs=1))
         ctx.enter_context(tc.manual_schedule())
 
-        t = {}
-
-        def unit_rows(rows, i):
-            return rows[UNIT * i : UNIT * (i + 1), :].rearrange("(p s) c -> p (s c)", s=2)
-
-        def load_x(i):
-            t["x", i] = work.tile([P, 2 * D], BF16, name="x_sb", bufs=4)
-            nc.sync.dma_start(out=t["x", i][:], in_=unit_rows(x_rows, i))
-
-        def load_err(i):
-            t["err", i] = work.tile([P, 2 * M], BF16, name="err_sb", bufs=4)
-            nc.sync.dma_start(out=t["err", i][:], in_=unit_rows(err_rows, i))
-
-        def load_c_words(g):
-            t["c_raw", g] = keep.tile([P, 2 * R], U8, name="c_raw%d" % g)
-            nc.sync.dma_start(out=t["c_raw", g][:].bitcast(I32), in_=c_words[g].bitcast(I32))
-
-        def load_scale_rows(plane, rows):
-            count = rows.shape[0]
-            for q in range(4):
-                nc.sync.dma_start(
-                    out=plane[32 * q : 32 * q + 4, :].bitcast(I32).rearrange("r (c n) -> r c n", c=count),
-                    in_=rows[:, 4 * q : 4 * q + 4, :].rearrange("c r n -> r c n").bitcast(I32),
-                )
-
-        def load_group(g):
-            t["f_words", g] = keep.tile([P, 4 * M], U8, name="f_words%d" % g, align_bytes=64)
-            nc.sync.dma_start(
-                out=t["f_words", g][:].bitcast(I32).rearrange("p (c n) -> p c n", c=2),
-                in_=f_words[2 * g : 2 * g + 2].rearrange("c p n -> p c n").bitcast(I32),
-            )
-
-        def load_u0(g):
-            t["u0", g] = keep.tile([P, M], BF16, name="u0_%d" % g)
-            nc.sync.dma_start(out=t["u0", g][:], in_=u0[g].partition_broadcast(P))
-
-        def sort_c_words(g, h):
-            if h == 0:
-                t["c", g] = keep.tile([P, 2 * R], U8, name="c_sorted%d" % g, align_bytes=64)
-            cols = slice(1024 * h, 1024 * (h + 1))
-            nc.vector.tensor_copy(
-                out=t["c", g][:, cols].rearrange("p (t m b) -> p t m b", t=4, b=2),
-                in_=t["c_raw", g][:, cols].rearrange("p (m t b) -> p t m b", t=4, b=2),
-            )
-
-        def sort_c_scales():
-            nc.vector.tensor_copy(
-                out=t["cs", 0].rearrange("p (h t m) -> p h t m", h=2, t=4),
-                in_=cs_packed[:].rearrange("p (h m t) -> p h t m", h=2, t=4),
-            )
-
-        def spread_c_scales(g):
-            for q in range(4):
-                nc.sync.dma_start(
-                    out=t["cs", g][32 * q : 32 * q + 4, :].bitcast(I32),
-                    in_=t["cs", 0][32 * q + 4 * g : 32 * q + 4 * g + 4, :].bitcast(I32),
-                )
-
-        def turn(src, bank):
-            words = src[:].bitcast(F32)
-            for s in range(2):
-                for u in range(2):
-                    nc.tensor.transpose(
-                        bank[:, P * (2 * s + u) : P * (2 * s + u + 1)],
-                        words[:, 256 * s + u : 256 * (s + 1) : 2],
-                        ident[:],
-                    )
-
-        def turn_x(i):
-            t["xT", i] = psum.tile([P, 512], F32, name="x_bank")
-            turn(t["x", i], t["xT", i])
-
-        def copy_x(i):
-            t["xb", i] = work.tile([P, 4 * UNIT], BF16, name="x_grouped", align_bytes=64)
-            nc.scalar.copy(
-                out=t["xb", i][:].bitcast(F32).rearrange("k (s p u) -> k s p u", s=2, u=2),
-                in_=t["xT", i][:].rearrange("k (s u p) -> k s p u", s=2, u=2),
-            )
-
-        def quantize_x(i):
-            t["xq", i] = work.tile([P, UNIT], U32, name="x_codes", bufs=3, align_bytes=64)
-            t["xs", i] = work.tile([P, UNIT], U8, name="x_scales", bufs=3, align_bytes=64)
-            nc.vector.quantize_mx(out=t["xq", i][:].bitcast(FP8X4), scales=t["xs", i][:], in_=t["xb", i][:])
-
-        def first_product(i, b):
-            g = i // PER_GROUP
-            h, s = divmod(b, 2)
-            t["S", i, b] = psum.tile([P, 512], F32, name="s_bank", bufs=3)
-            for slot in range(4):
-                col = 4 * h + slot
-                nc.tensor.matmul_mx(
-                    out=t["S", i, b][:, P * slot : P * (slot + 1)],
-                    lhsT=t["c", g][:, 2 * P * col : 2 * P * (col + 1)].bitcast(FP4X4),
-                    lhsT_scale=t["cs", g][:, P * col : P * (col + 1)],
-                    rhs=t["xq", i][:, P * s : P * (s + 1)].bitcast(FP8X4),
-                    rhs_scale=t["xs", i][:, P * s : P * (s + 1)],
-                    start=True,
-                    stop=True,
-                )
-
-        def exponential(i, b):
-            h, s = divmod(b, 2)
-            if s == 0:
-                t["E", i, h] = work.tile([P, 1024], F32, name="exp_s", bufs=4)
-            nc.scalar.activation(
-                out=t["E", i, h][:, 512 * s : 512 * (s + 1)].rearrange("p (n t) -> p n t", t=4),
-                in_=t["S", i, b][:].rearrange("p (t n) -> p n t", t=4),
-                func=ACT.Exp,
-            )
-
-        def times_rulefac(i, h):
-            row = 2 * (i // PER_GROUP) + h
-            if h == 0:
-                t["H", i] = work.tile([P, 8 * UNIT], BF16, name="h_grouped", align_bytes=64)
-            nc.vector.tensor_tensor(
-                out=t["H", i][:, 1024 * h : 1024 * (h + 1)].rearrange("p (n t) -> p n t", t=4),
-                in0=t["E", i, h][:].rearrange("p (n t) -> p n t", t=4),
-                in1=rule_quads[:, 4 * row : 4 * row + 4].unsqueeze(1).to_broadcast([P, UNIT, 4]),
-                op=ALU.mult,
-            )
-
-        def quantize_h(i):
-            t["hq", i] = work.tile([P, 2 * UNIT], U32, name="h_codes", bufs=3, align_bytes=64)
-            t["hs", i] = work.tile([P, 2 * UNIT], U8, name="h_scales", bufs=3, align_bytes=64)
-            nc.vector.quantize_mx(out=t["hq", i][:].bitcast(FP8X4), scales=t["hs", i][:], in_=t["H", i][:])
-
-        def second_product(i, s):
-            g = i // PER_GROUP
-            t["U", i, s] = psum.tile([P, M], F32, name="u_bank", bufs=2)
-            for h in range(2):
-                cols = slice(UNIT * h + P * s, UNIT * h + P * (s + 1))
-                nc.tensor.matmul_mx(
-                    out=t["U", i, s][:],
-                    lhsT=t["hq", i][:, cols].bitcast(FP8X4),
-                    lhsT_scale=t["hs", i][:, cols],
-                    rhs=t["f_words", g][:, 2 * M * h : 2 * M * (h + 1)].bitcast(FP4X4),
-                    rhs_scale=f_plane[:, M * (2 * g + h) : M * (2 * g + h + 1)],
-                    start=(h == 0),
-                    stop=(h == 1),
-                )
-
-        def times_err(i, s):
-            t["V", i, s] = work.tile([P, M], F32, name="gain_err", bufs=4)
-            nc.vector.scalar_tensor_tensor(
-                out=t["V", i, s][:],
-                in0=t["err", i][:, M * s : M * (s + 1)],
-                scalar=row_f32[:, 2 * i + s : 2 * i + s + 1],
-                in1=t["U", i, s][:],
-                op0=ALU.mult,
-                op1=ALU.mult,
-            )
-
-        def add_u0(engine, i, s):
-            if s == 0:
-                t["y", i] = work.tile([P, 2 * M], F32, name="y_sb", bufs=4)
-                t["yb", i] = work.tile([P, 2 * M], BF16, name="y_bf16", bufs=3)
-            engine.tensor_tensor(
-                out=t["y", i][:, M * s : M * (s + 1)],
-                in0=t["V", i, s][:],
-                in1=t["u0", i // PER_GROUP][:],
-                op=ALU.add,
-            )
-
-        def store_y(i, cols):
-            nc.sync.dma_start(out=unit_rows(y_rows, i)[:, cols], in_=t["y", i][:, cols])
-
-        def round_y(copy, i, cols):
-            copy(out=t["yb", i][:, cols], in_=t["y", i][:, cols])
-
-        def turn_y(i, bank_name):
-            t["yT", i] = psum.tile([P, 512], F32, name=bank_name)
-            turn(t["yb", i], t["yT", i])
-
-        def copy_y(i):
-            t["yg", i] = work.tile([P, 4 * UNIT], BF16, name="y_grouped", align_bytes=64)
-            nc.scalar.copy(
-                out=t["yg", i][:].bitcast(F32).rearrange("k (p s u) -> k p s u", s=2, u=2),
-                in_=t["yT", i][:].rearrange("k (s u p) -> k p s u", s=2, u=2),
-            )
-
-        def quantize_y(i):
-            g, j = divmod(i, PER_GROUP)
-            if i % 2 == 0:
-                t["yq", i // 2] = work.tile([P, 2 * UNIT], U32, name="y_codes", bufs=3, align_bytes=64)
-            if j == 0:
-                t["ys", g] = work.tile([P, N], U8, name="y_scales", align_bytes=64)
-            codes = t["yq", i // 2]
-            nc.vector.quantize_mx(
-                out=codes[:, UNIT * (i % 2) : UNIT * (i % 2 + 1)].bitcast(FP8X4),
-                scales=t["ys", g][:, UNIT * j : UNIT * (j + 1)],
-                in_=t["yg", i][:],
-            )
-            if i >= UNITS - 2:
-                nc.sync.dma_start(
-                    out=out_words[:, UNIT * i : UNIT * (i + 1)],
-                    in_=codes[:, UNIT * (i % 2) : UNIT * (i % 2 + 1)].bitcast(I32),
-                )
-            elif i % 2 == 1:
-                nc.sync.dma_start(out=out_words[:, UNIT * (i - 1) : UNIT * (i + 1)], in_=codes[:].bitcast(I32))
-            if j == PER_GROUP - 1:
-                for q in range(4):
-                    (nc.scalar if g == G - 1 and q % 2 else nc.sync).dma_start(
-                        out=out_2[0, 4 * q : 4 * q + 4, N * g : N * (g + 1)].bitcast(I32),
-                        in_=t["ys", g][32 * q : 32 * q + 4, :].bitcast(I32),
-                    )
-
-        ident = keep.tile([P, P], F32)
-        cs_packed = keep.tile([P, R], U8)
-        cs_first = keep.tile([P, R], U8, align_bytes=64)
-        cs_rest = keep.tile([P, (G - 1) * R], U8, align_bytes=64)
-        f_plane = keep.tile([P, 2 * G * M], U8, align_bytes=64)
-        rule_rows = keep.tile([P, 512], BF16)
-        row_bf16 = keep.tile([P, 2 * UNITS], BF16)
-        row_f32 = keep.tile([P, 2 * UNITS], F32)
-        warm = keep.tile([P, 2], F32)
-
-        nc.vector.memset(cs_packed[:].bitcast(I32), 0)
-        nc.vector.memset(warm[:], 0.0)
-        nc.scalar.activation(out=warm[:, 1:2], in_=warm[:, 0:1], func=ACT.Exp)
-        nc.vector.memset(rule_rows[:], 0.0)
-        make_identity(nc, ident[:])
-        nc.vector.memset(cs_rest[:].bitcast(I32), 0)
-        nc.vector.memset(f_plane[:].bitcast(I32), 0)
-
-        t["cs", 0] = cs_first[:]
-        for g in range(1, G):
-            t["cs", g] = cs_rest[:, R * (g - 1) : R * g]
-
-        load_x(0)
-        load_c_words(0)
-        for q in range(4):
-            nc.sync.dma_start(
-                out=cs_packed[32 * q : 32 * q + 4 * G, :].bitcast(I32),
-                in_=c_scales[:, 4 * q : 4 * q + 4, :].bitcast(I32),
-            )
-        nc.sync.dma_start(out=rule_rows[0 : 2 * G, :], in_=rulefac.rearrange("g (h r) -> (g h) r", h=2))
-        load_x(1)
-        load_c_words(1)
-        load_x(2)
-        load_group(0)
-        load_scale_rows(f_plane, f_scales)
-        nc.sync.dma_start(
-            out=row_bf16[:].rearrange("p (i s) -> p i s", s=2),
-            in_=rowfac.rearrange("g (j p s) -> p (g j) s", p=P, s=2),
-        )
-        load_u0(0)
-
-        turn_x(0)
-        rule_bank = psum.tile([P, 512], F32)
-        rule_words = rule_rows[:].bitcast(F32)
-        for u in range(2):
-            nc.tensor.transpose(rule_bank[:, u : 2 * P : 2], rule_words[:, u : 256 : 2], ident[:])
-        rule_quads = rule_bank[:].bitcast(BF16)
-        nc.gpsimd.tensor_copy(out=row_f32[:], in_=row_bf16[:])
-        sort_c_words(0, 0)
-        sort_c_scales()
-        sort_c_words(0, 1)
+        tiles = {}
 
         def live(i):
             return 0 <= i < UNITS
 
-        sort_at = {-2: (1, 0), -1: (1, 1), 3: (2, 0), 4: (2, 1), 7: (3, 0), 8: (3, 1)}
+        def unit_rows(rows, i):
+            return rows[UNIT * i : UNIT * (i + 1), :].rearrange("(p r) c -> p (r c)", r=HALVES)
 
-        def fill(n):
-            if 0 <= n < 4 * UNITS:
-                first_product(n // 4, n % 4)
+        def half_cols(first, count):
+            return slice(M * first, M * (first + count))
 
-        def drain(n):
-            if 0 <= n < 4 * UNITS:
-                exponential(n // 4, n % 4)
 
-        whole = slice(0, 2 * M)
-        half = [slice(0, M), slice(M, 2 * M)]
+        def load_x(i):
+            tiles["x", i] = work.tile([P, HALVES * D], BF16, name="x_sb", bufs=4)
+            nc.sync.dma_start(out=tiles["x", i][:], in_=unit_rows(x_rows, i))
 
-        for s in range(-2, UNITS):
-            if live(s + 5):
-                load_x(s + 5)
+        def load_err(i):
+            tiles["err", i] = work.tile([P, HALVES * M], BF16, name="err_sb", bufs=4)
+            nc.sync.dma_start(out=tiles["err", i][:], in_=unit_rows(err_rows, i))
+
+        def load_c_words(g):
+            tiles["c_raw", g] = keep.tile([P, FP4_WORD * R], U8, name="c_raw%d" % g)
+            nc.sync.dma_start(out=tiles["c_raw", g][:].bitcast(I32), in_=c_words[g].bitcast(I32))
+
+        def load_f_words(g):
+            tiles["f", g] = keep.tile([P, RULE_PASSES * FP4_WORD * M], U8, name="f_words%d" % g, align_bytes=64)
+            nc.sync.dma_start(
+                out=tiles["f", g][:].bitcast(I32).rearrange("p (h n) -> p h n", h=RULE_PASSES),
+                in_=f_words[RULE_PASSES * g : RULE_PASSES * (g + 1)].rearrange("h p n -> p h n").bitcast(I32),
+            )
+
+        def load_u0(g):
+            tiles["u0", g] = keep.tile([P, M], BF16, name="u0_%d" % g)
+            nc.sync.dma_start(out=tiles["u0", g][:], in_=u0[g].partition_broadcast(P))
+
+
+        def sort_c_words(g, h):
+            if h == 0:
+                tiles["c", g] = keep.tile([P, FP4_WORD * R], U8, name="c_sorted%d" % g, align_bytes=64)
+            cols = slice(FP4_WORD * K_PASS * h, FP4_WORD * K_PASS * (h + 1))
+            nc.vector.tensor_copy(
+                out=tiles["c", g][:, cols].rearrange("p (t m b) -> p t m b", t=PACK, b=FP4_WORD),
+                in_=tiles["c_raw", g][:, cols].rearrange("p (m t b) -> p t m b", t=PACK, b=FP4_WORD),
+            )
+
+        def sort_c_scales():
+            nc.vector.tensor_copy(
+                out=tiles["c_plane", 0].rearrange("p (h t m) -> p h t m", h=RULE_PASSES, t=PACK),
+                in_=c_scale_rows[:].rearrange("p (h m t) -> p h t m", h=RULE_PASSES, t=PACK),
+            )
+
+        def spread_c_scales(g):
+            for q in range(QUADRANTS):
+                nc.sync.dma_start(
+                    out=tiles["c_plane", g][32 * q : 32 * q + 4, :].bitcast(I32),
+                    in_=tiles["c_plane", 0][32 * q + 4 * g : 32 * q + 4 * g + 4, :].bitcast(I32),
+                )
+
+
+        def turn(src, bank, halves):
+            pairs = src[:].bitcast(F32)
+            per_half = K_PASS // 2
+            for r in halves:
+                for u in range(2):
+                    nc.tensor.transpose(
+                        bank[:, P * (2 * r + u) : P * (2 * r + u + 1)],
+                        pairs[:, per_half * r + u : per_half * (r + 1) : 2],
+                        ident[:],
+                    )
+
+        def turn_x(i, bank_name):
+            tiles["xT", i] = psum.tile([P, BANK], F32, name=bank_name)
+            turn(tiles["x", i], tiles["xT", i], range(HALVES))
+
+        def copy_x(i):
+            tiles["xg", i] = work.tile([P, PACK * UNIT], BF16, name="x_grouped", align_bytes=64)
+            nc.scalar.copy(
+                out=tiles["xg", i][:].bitcast(F32).rearrange("k (r p u) -> k r p u", r=HALVES, u=2),
+                in_=tiles["xT", i][:].rearrange("k (r u p) -> k r p u", r=HALVES, u=2),
+            )
+
+        def quantize_x(i):
+            tiles["xq", i] = work.tile([P, UNIT], U32, name="x_codes", bufs=3, align_bytes=64)
+            tiles["xs", i] = work.tile([P, UNIT], U8, name="x_scales", bufs=3, align_bytes=64)
+            nc.vector.quantize_mx(
+                out=tiles["xq", i][:].bitcast(FP8X4), scales=tiles["xs", i][:], in_=tiles["xg", i][:]
+            )
+
+
+        def first_product(n):
+            if n >= S_TILES * UNITS:
+                return
+            i, (h, r) = n // S_TILES, divmod(n % S_TILES, HALVES)
+            g = i // PER_GROUP
+            samples = slice(P * r, P * (r + 1))
+            tiles["S", n] = psum.tile([P, BANK], F32, name="s_bank", bufs=S_BANKS)
+            for t in range(PACK):
+                slot = PACK * h + t
+                nc.tensor.matmul_mx(
+                    out=tiles["S", n][:, P * t : P * (t + 1)],
+                    lhsT=tiles["c", g][:, FP4_WORD * P * slot : FP4_WORD * P * (slot + 1)].bitcast(FP4X4),
+                    lhsT_scale=tiles["c_plane", g][:, P * slot : P * (slot + 1)],
+                    rhs=tiles["xq", i][:, samples].bitcast(FP8X4),
+                    rhs_scale=tiles["xs", i][:, samples],
+                    start=True,
+                    stop=True,
+                )
+
+        def exponential(n):
+            if n >= S_TILES * UNITS:
+                return
+            i, (h, r) = n // S_TILES, divmod(n % S_TILES, HALVES)
+            if r == 0:
+                tiles["E", i, h] = work.tile([P, PACK * UNIT], F32, name="exp_s", bufs=4)
+            nc.scalar.activation(
+                out=tiles["E", i, h][:, BANK * r : BANK * (r + 1)].rearrange("p (n t) -> p n t", t=PACK),
+                in_=tiles["S", n][:].rearrange("p (t n) -> p n t", t=PACK),
+                func=ACT.Exp,
+            )
+
+        def times_rulefac(i, h):
+            row = RULE_PASSES * (i // PER_GROUP) + h
+            if h == 0:
+                tiles["H", i] = work.tile([P, RULE_PASSES * PACK * UNIT], BF16, name="h_grouped", align_bytes=64)
+            nc.vector.tensor_tensor(
+                out=tiles["H", i][:, PACK * UNIT * h : PACK * UNIT * (h + 1)].rearrange("p (n t) -> p n t", t=PACK),
+                in0=tiles["E", i, h][:].rearrange("p (n t) -> p n t", t=PACK),
+                in1=rule_quads[:, PACK * row : PACK * (row + 1)].unsqueeze(1).to_broadcast([P, UNIT, PACK]),
+                op=ALU.mult,
+            )
+
+        def quantize_h(i):
+            tiles["hq", i] = work.tile([P, RULE_PASSES * UNIT], U32, name="h_codes", bufs=3, align_bytes=64)
+            tiles["hs", i] = work.tile([P, RULE_PASSES * UNIT], U8, name="h_scales", bufs=3, align_bytes=64)
+            nc.vector.quantize_mx(
+                out=tiles["hq", i][:].bitcast(FP8X4), scales=tiles["hs", i][:], in_=tiles["H", i][:]
+            )
+
+
+        def second_product(i, r, bank_name, banks):
+            g = i // PER_GROUP
+            tiles["U", i, r] = psum.tile([P, BANK], F32, name=bank_name, bufs=banks)
+            for h in range(RULE_PASSES):
+                samples = slice(UNIT * h + P * r, UNIT * h + P * (r + 1))
+                f_pass = RULE_PASSES * g + h
+                nc.tensor.matmul_mx(
+                    out=tiles["U", i, r][:],
+                    lhsT=tiles["hq", i][:, samples].bitcast(FP8X4),
+                    lhsT_scale=tiles["hs", i][:, samples],
+                    rhs=tiles["f", g][:, FP4_WORD * M * h : FP4_WORD * M * (h + 1)].bitcast(FP4X4),
+                    rhs_scale=f_plane[:, M * f_pass : M * (f_pass + 1)],
+                    start=(h == 0),
+                    stop=(h == RULE_PASSES - 1),
+                )
+
+        def times_err(i, r):
+            if r == 0:
+                tiles["V", i] = work.tile([P, HALVES * M], F32, name="gain_err", bufs=3)
+                tiles["y", i] = work.tile([P, HALVES * M], F32, name="y_sb", bufs=4)
+                tiles["yb", i] = work.tile([P, HALVES * M], BF16, name="y_bf16", bufs=3)
+            nc.vector.scalar_tensor_tensor(
+                out=tiles["V", i][:, half_cols(r, 1)],
+                in0=tiles["err", i][:, half_cols(r, 1)],
+                scalar=row_f32[:, HALVES * i + r : HALVES * i + r + 1],
+                in1=tiles["U", i, r][:],
+                op0=ALU.mult,
+                op1=ALU.mult,
+            )
+
+        def add_u0_and_store(engine, i, first, count):
+            cols = half_cols(first, count)
+            engine.tensor_tensor(
+                out=tiles["y", i][:, cols].rearrange("p (r j) -> p r j", r=count),
+                in0=tiles["V", i][:, cols].rearrange("p (r j) -> p r j", r=count),
+                in1=tiles["u0", i // PER_GROUP][:].unsqueeze(1).to_broadcast([P, count, M]),
+                op=ALU.add,
+            )
+            nc.sync.dma_start(out=unit_rows(y_rows, i)[:, cols], in_=tiles["y", i][:, cols])
+
+        def round_y(copy, i, first, count):
+            cols = half_cols(first, count)
+            copy(out=tiles["yb", i][:, cols], in_=tiles["y", i][:, cols])
+
+        def turn_y(i, bank_name, halves):
+            tiles["yT", i] = psum.tile([P, BANK], F32, name=bank_name)
+            turn(tiles["yb", i], tiles["yT", i], halves)
+
+        def copy_y(i):
+            tiles["yg", i] = work.tile([P, PACK * UNIT], BF16, name="y_grouped", align_bytes=64)
+            nc.scalar.copy(
+                out=tiles["yg", i][:].bitcast(F32).rearrange("k (p r u) -> k p r u", r=HALVES, u=2),
+                in_=tiles["yT", i][:].rearrange("k (r u p) -> k p r u", r=HALVES, u=2),
+            )
+
+        def quantize_y(i):
+            g, j = divmod(i, PER_GROUP)
+            pair, place = divmod(i, 2)
+            if place == 0:
+                tiles["yq", pair] = work.tile([P, 2 * UNIT], U32, name="y_codes", bufs=3, align_bytes=64)
+            if j == 0:
+                tiles["ys", g] = work.tile([P, N], U8, name="y_scales", align_bytes=64)
+            codes = tiles["yq", pair]
+            own = slice(UNIT * place, UNIT * (place + 1))
+            nc.vector.quantize_mx(
+                out=codes[:, own].bitcast(FP8X4),
+                scales=tiles["ys", g][:, UNIT * j : UNIT * (j + 1)],
+                in_=tiles["yg", i][:],
+            )
+            if i >= UNITS - 2:
+                nc.sync.dma_start(out=out_words[:, UNIT * i : UNIT * (i + 1)], in_=codes[:, own].bitcast(I32))
+            elif place == 1:
+                nc.sync.dma_start(out=out_words[:, UNIT * (i - 1) : UNIT * (i + 1)], in_=codes[:].bitcast(I32))
+            if j == PER_GROUP - 1:
+                for q in range(QUADRANTS):
+                    queue = nc.scalar if g == G - 1 and q % 2 == 1 else nc.sync
+                    queue.dma_start(
+                        out=out_2[0, 4 * q : 4 * q + 4, N * g : N * (g + 1)].bitcast(I32),
+                        in_=tiles["ys", g][32 * q : 32 * q + 4, :].bitcast(I32),
+                    )
+
+        ident = keep.tile([P, P], F32)
+        c_scale_rows = keep.tile([P, R], U8)
+        c_plane_first = keep.tile([P, R], U8, align_bytes=64)
+        c_plane_rest = keep.tile([P, (G - 1) * R], U8, align_bytes=64)
+        f_plane = keep.tile([P, G * RULE_PASSES * M], U8, align_bytes=64)
+        rule_rows = keep.tile([P, K_PASS], BF16)
+        row_bf16 = keep.tile([P, HALVES * UNITS], BF16)
+        row_f32 = keep.tile([P, HALVES * UNITS], F32)
+
+        nc.vector.memset(c_scale_rows[:].bitcast(I32), 0)
+        nc.vector.memset(rule_rows[:], 0.0)
+        make_identity(nc, ident[:])
+        nc.vector.memset(c_plane_rest[:].bitcast(I32), 0)
+        nc.vector.memset(f_plane[:].bitcast(I32), 0)
+
+        tiles["c_plane", 0] = c_plane_first[:]
+        for g in range(1, G):
+            tiles["c_plane", g] = c_plane_rest[:, R * (g - 1) : R * g]
+
+        load_x(0)
+        load_c_words(0)
+        for q in range(QUADRANTS):
+            nc.sync.dma_start(
+                out=c_scale_rows[32 * q : 32 * q + 4 * G, :].bitcast(I32),
+                in_=c_scales[:, 4 * q : 4 * q + 4, :].bitcast(I32),
+            )
+        load_x(1)
+        nc.sync.dma_start(
+            out=rule_rows[0 : G * RULE_PASSES, :], in_=rulefac.rearrange("g (h k) -> (g h) k", h=RULE_PASSES)
+        )
+        load_x(2)
+        load_c_words(1)
+        load_f_words(0)
+        for q in range(QUADRANTS):
+            nc.sync.dma_start(
+                out=f_plane[32 * q : 32 * q + 4, :].bitcast(I32).rearrange("s (c n) -> s c n", c=G * RULE_PASSES),
+                in_=f_scales[:, 4 * q : 4 * q + 4, :].rearrange("c s n -> s c n").bitcast(I32),
+            )
+        load_x(3)
+        nc.sync.dma_start(
+            out=row_bf16[:].rearrange("p (i r) -> p i r", r=HALVES),
+            in_=rowfac.rearrange("g (j p r) -> p (g j) r", p=P, r=HALVES),
+        )
+        load_u0(0)
+        load_err(0)
+
+        turn_x(0, "x_bank")
+        turn_x(1, "y_bank")
+        load_x(4)
+        rule_bank = psum.tile([P, BANK], F32)
+        rule_pairs = rule_rows[:].bitcast(F32)
+        for u in range(2):
+            nc.tensor.transpose(rule_bank[:, u : 2 * P : 2], rule_pairs[:, u : K_PASS // 2 : 2], ident[:])
+        rule_quads = rule_bank[:].bitcast(BF16)
+        nc.gpsimd.tensor_copy(out=row_f32[:], in_=row_bf16[:])
+        sort_c_words(0, 0)
+        sort_c_scales()
+        copy_x(0)
+        quantize_x(0)
+        sort_c_words(0, 1)
+        copy_x(1)
+        for n in range(S_BANKS):
+            first_product(n)
+        quantize_x(1)
+        for h in range(RULE_PASSES):
+            sort_c_words(1, h)
+        for n in range(S_TILES):
+            exponential(n)
+            first_product(n + S_BANKS)
+            if n == 1:
+                turn_x(2, "x_bank")
+
+        for s in range(UNITS):
+            g, j = divmod(s, PER_GROUP)
+            n = S_TILES * (s + 1)
+            if live(s + X_AHEAD):
+                load_x(s + X_AHEAD)
             if live(s + 1):
                 load_err(s + 1)
-            if s in (0, 4):
-                load_c_words(s // 4 + 2)
-            if s in (1, 5, 9):
-                load_group(s // 4 + 1)
-                load_u0(s // 4 + 1)
-            if s in (0, 3, 6):
-                spread_c_scales(s // 3 + 1)
+            if j == 0 and g + 2 < G:
+                load_c_words(g + 2)
+            if j == 0 and g + 1 < G:
+                spread_c_scales(g + 1)
+            if j == 1 and g + 1 < G:
+                load_f_words(g + 1)
+                load_u0(g + 1)
+
+            if live(s - 1):
+                second_product(s - 1, 0, "u_bank", U_BANKS)
             if live(s - 2):
-                for r in range(2):
-                    times_err(s - 2, r)
-                for r in range(2):
-                    add_u0(nc.gpsimd, s - 2, r)
-                store_y(s - 2, whole)
+                times_err(s - 2, 1)
+                add_u0_and_store(nc.gpsimd, s - 2, 0, HALVES)
             if live(s - 3):
-                round_y(nc.scalar.copy, s - 3, whole)
+                round_y(nc.scalar.copy, s - 3, 0, HALVES)
             if live(s + 2):
                 copy_x(s + 2)
-            if live(s - 1):
-                second_product(s - 1, 0)
             if live(s - 3):
-                turn_y(s - 3, "y_bank")
+                turn_y(s - 3, "y_bank", range(HALVES))
             if live(s + 3):
-                turn_x(s + 3)
+                turn_x(s + 3, "x_bank")
             if live(s - 1):
-                second_product(s - 1, 1)
-            if live(s):
-                times_rulefac(s, 0)
-                times_rulefac(s, 1)
-            drain(4 * s + 4)
-            fill(4 * s + 7)
-            drain(4 * s + 5)
+                second_product(s - 1, 1, "u_bank", U_BANKS)
+            for h in range(RULE_PASSES):
+                times_rulefac(s, h)
+            if live(s - 1):
+                times_err(s - 1, 0)
+            exponential(n)
+            first_product(n + S_BANKS)
+            exponential(n + 1)
             if live(s - 3):
                 copy_y(s - 3)
             if live(s + 2):
                 quantize_x(s + 2)
-            if s in sort_at:
-                sort_c_words(*sort_at[s])
-            if live(s):
-                quantize_h(s)
+            sort_group, sort_pass = divmod(s + 5, PER_GROUP)
+            if 2 <= sort_group < G and sort_pass < RULE_PASSES:
+                sort_c_words(sort_group, sort_pass)
+            quantize_h(s)
             if live(s - 3):
                 quantize_y(s - 3)
-            fill(4 * s + 8)
-            drain(4 * s + 6)
-            fill(4 * s + 9)
-            drain(4 * s + 7)
-            fill(4 * s + 10)
+            first_product(n + 1 + S_BANKS)
+            for later in (n + 2, n + 3):
+                exponential(later)
+                first_product(later + S_BANKS)
 
-        a, b, c = UNITS - 3, UNITS - 2, UNITS - 1
-        times_err(b, 0)
-        times_err(b, 1)
-        add_u0(nc.gpsimd, b, 0)
-        store_y(b, half[0])
-        round_y(nc.scalar.copy, a, whole)
-        second_product(c, 0)
-        second_product(c, 1)
-        turn_y(a, "y_bank")
-        times_err(c, 0)
-        times_err(c, 1)
-        copy_y(a)
-        for i, r in ((b, 1), (c, 0), (c, 1)):
-            add_u0(nc.vector, i, r)
-            store_y(i, half[r])
-        for i, r in ((b, 0), (b, 1), (c, 0)):
-            round_y(nc.scalar.copy, i, half[r])
-        turn_y(b, "y_bank")
-        quantize_y(a)
-        round_y(nc.vector.tensor_copy, c, half[1])
-        turn_y(c, "x_bank")
-        for i in (b, c):
+        third_last, second_last, last = UNITS - 3, UNITS - 2, UNITS - 1
+        second_product(last, 0, "u_bank", U_BANKS)
+        second_product(last, 1, "s_bank", S_BANKS)
+        times_err(second_last, 1)
+        add_u0_and_store(nc.gpsimd, second_last, 1, 1)
+        round_y(nc.scalar.copy, third_last, 0, HALVES)
+        turn_y(third_last, "y_bank", range(HALVES))
+        for r in range(HALVES):
+            times_err(last, r)
+        copy_y(third_last)
+        for i, r in ((second_last, 0), (last, 0), (last, 1)):
+            add_u0_and_store(nc.vector, i, r, 1)
+        for r in (1, 0):
+            round_y(nc.scalar.copy, second_last, r, 1)
+        turn_y(second_last, "y_bank", (1, 0))
+        for r in range(HALVES):
+            round_y(nc.vector.tensor_copy, last, r, 1)
+        turn_y(last, "x_bank", range(HALVES))
+        quantize_y(third_last)
+        for i in (second_last, last):
             copy_y(i)
             quantize_y(i)

@@ -235,7 +235,7 @@ def tile_takagi_sugeno_gain_blend_k7_kernel(
             turn(tiles["yb", i], tiles["yT", i], halves)
 
         def copy_y(i):
-            tiles["yg", i] = work.tile([P, PACK * UNIT], BF16, name="y_grouped", align_bytes=64)
+            tiles["yg", i] = work.tile([P, PACK * UNIT], BF16, name="y_grouped", bufs=3, align_bytes=64)
             nc.scalar.copy(
                 out=tiles["yg", i][:].bitcast(F32).rearrange("k (p r u) -> k p r u", r=HALVES, u=2),
                 in_=tiles["yT", i][:].rearrange("k (r u p) -> k p r u", r=HALVES, u=2),
@@ -299,6 +299,7 @@ def tile_takagi_sugeno_gain_blend_k7_kernel(
         )
         load_x(2)
         load_c_words(1)
+        load_c_words(2)
         load_f_words(0)
         for q in range(QUADRANTS):
             nc.sync.dma_start(
@@ -333,11 +334,14 @@ def tile_takagi_sugeno_gain_blend_k7_kernel(
         quantize_x(1)
         for h in range(RULE_PASSES):
             sort_c_words(1, h)
+        sort_c_words(2, 0)
         for n in range(S_TILES):
             exponential(n)
             first_product(n + S_BANKS)
             if n == 1:
                 turn_x(2, "x_bank")
+                times_rulefac(0, 0)
+                sort_c_words(2, 1)
 
         for s in range(UNITS):
             g, j = divmod(s, PER_GROUP)
@@ -346,8 +350,8 @@ def tile_takagi_sugeno_gain_blend_k7_kernel(
                 load_x(s + X_AHEAD)
             if live(s + 1):
                 load_err(s + 1)
-            if j == 0 and g + 2 < G:
-                load_c_words(g + 2)
+            if s == 0:
+                load_c_words(G - 1)
             if j == 0 and g + 1 < G:
                 spread_c_scales(g + 1)
             if j == 1 and g + 1 < G:
@@ -369,7 +373,7 @@ def tile_takagi_sugeno_gain_blend_k7_kernel(
                 turn_x(s + 3, "x_bank")
             if live(s - 1):
                 second_product(s - 1, 1, "u_bank", U_BANKS)
-            for h in range(RULE_PASSES):
+            for h in range(1 if s == 0 else 0, RULE_PASSES):
                 times_rulefac(s, h)
             if live(s - 1):
                 times_err(s - 1, 0)
@@ -380,12 +384,11 @@ def tile_takagi_sugeno_gain_blend_k7_kernel(
                 copy_y(s - 3)
             if live(s + 2):
                 quantize_x(s + 2)
-            sort_group, sort_pass = divmod(s + 5, PER_GROUP)
-            if 2 <= sort_group < G and sort_pass < RULE_PASSES:
-                sort_c_words(sort_group, sort_pass)
+            if g == 1 and j < RULE_PASSES:
+                sort_c_words(G - 1, j)
             quantize_h(s)
-            if live(s - 3):
-                quantize_y(s - 3)
+            if live(s - 4):
+                quantize_y(s - 4)
             first_product(n + 1 + S_BANKS)
             for later in (n + 2, n + 3):
                 exponential(later)
@@ -409,7 +412,8 @@ def tile_takagi_sugeno_gain_blend_k7_kernel(
         for r in range(HALVES):
             round_y(nc.vector.tensor_copy, last, r, 1)
         turn_y(last, "x_bank", range(HALVES))
-        quantize_y(third_last)
+        for i in (third_last - 1, third_last):
+            quantize_y(i)
         for i in (second_last, last):
             copy_y(i)
             quantize_y(i)

from contextlib import ExitStack

import concourse.mybir as mybir
from concourse.masks import make_identity

F32 = mybir.dt.float32
BF16 = mybir.dt.bfloat16
I32 = mybir.dt.int32
U32 = mybir.dt.uint32
U8 = mybir.dt.uint8
FP8X4 = mybir.dt.float8_e4m3fn_x4
FP4X4 = mybir.dt.float4_e2m1fn_x4
ALU = mybir.AluOpType
ACT = mybir.ActivationFunctionType

G, N, D, R, M = 4, 1024, 512, 1024, 512
P = 128
PACK = 4
K_PASS = P * PACK
BANK = 512
FP4_WORD = 2
QUADRANTS = 4
HALVES = 2
UNIT = P * HALVES
UNITS = G * N // UNIT
PER_GROUP = N // UNIT
RULE_PASSES = R // K_PASS
S_TILES = RULE_PASSES * HALVES
S_BANKS = 3
U_BANKS = 2
X_AHEAD = 5
FLOPS = 2 * G * N * D * R + 2 * G * N * R * M


def tile_takagi_sugeno_gain_blend_k7_kernel(
    tc, x, c_words, c_scales, rulefac, f_words, f_scales, rowfac, err, u0, out_0, out_1, out_2
):
    nc = tc.nc
    x_rows = x.rearrange("g n d -> (g n) d")
    err_rows = err.rearrange("g n j -> (g n) j")
    y_rows = out_0.rearrange("g n j -> (g n) j")
    out_words = out_1[0].rearrange("p m t -> p (m t)").bitcast(I32)

    with ExitStack() as ctx:
        keep = ctx.enter_context(tc.tile_pool(name="keep", bufs=1))
        work = ctx.enter_context(tc.tile_pool(name="work", bufs=2))
        psum = ctx.enter_context(tc.psum_pool(name="psum", bufs=1))
        ctx.enter_context(tc.manual_schedule())

        tiles = {}

        def live(i):
            return 0 <= i < UNITS

        def unit_rows(rows, i):
            return rows[UNIT * i : UNIT * (i + 1), :].rearrange("(p r) c -> p (r c)", r=HALVES)

        def half_cols(first, count):
            return slice(M * first, M * (first + count))


        def load_x(i):
            tiles["x", i] = work.tile([P, HALVES * D], BF16, name="x_sb", bufs=4)
            nc.sync.dma_start(out=tiles["x", i][:], in_=unit_rows(x_rows, i))

        def load_err(i):
            tiles["err", i] = work.tile([P, HALVES * M], BF16, name="err_sb", bufs=4)
            nc.sync.dma_start(out=tiles["err", i][:], in_=unit_rows(err_rows, i))

        def load_c_words(g):
            tiles["c_raw", g] = keep.tile([P, FP4_WORD * R], U8, name="c_raw%d" % g)
            nc.sync.dma_start(out=tiles["c_raw", g][:].bitcast(I32), in_=c_words[g].bitcast(I32))

        def load_f_words(g):
            tiles["f", g] = keep.tile([P, RULE_PASSES * FP4_WORD * M], U8, name="f_words%d" % g, align_bytes=64)
            nc.sync.dma_start(
                out=tiles["f", g][:].bitcast(I32).rearrange("p (h n) -> p h n", h=RULE_PASSES),
                in_=f_words[RULE_PASSES * g : RULE_PASSES * (g + 1)].rearrange("h p n -> p h n").bitcast(I32),
            )

        def load_u0(g):
            tiles["u0", g] = keep.tile([P, M], BF16, name="u0_%d" % g)
            nc.sync.dma_start(out=tiles["u0", g][:], in_=u0[g].partition_broadcast(P))


        def sort_c_words(g, h):
            if h == 0:
                tiles["c", g] = keep.tile([P, FP4_WORD * R], U8, name="c_sorted%d" % g, align_bytes=64)
            cols = slice(FP4_WORD * K_PASS * h, FP4_WORD * K_PASS * (h + 1))
            nc.vector.tensor_copy(
                out=tiles["c", g][:, cols].rearrange("p (t m b) -> p t m b", t=PACK, b=FP4_WORD),
                in_=tiles["c_raw", g][:, cols].rearrange("p (m t b) -> p t m b", t=PACK, b=FP4_WORD),
            )

        def sort_c_scales():
            nc.vector.tensor_copy(
                out=tiles["c_plane", 0].rearrange("p (h t m) -> p h t m", h=RULE_PASSES, t=PACK),
                in_=c_scale_rows[:].rearrange("p (h m t) -> p h t m", h=RULE_PASSES, t=PACK),
            )

        def spread_c_scales(g):
            for q in range(QUADRANTS):
                nc.sync.dma_start(
                    out=tiles["c_plane", g][32 * q : 32 * q + 4, :].bitcast(I32),
                    in_=tiles["c_plane", 0][32 * q + 4 * g : 32 * q + 4 * g + 4, :].bitcast(I32),
                )


        def turn(src, bank, halves):
            pairs = src[:].bitcast(F32)
            per_half = K_PASS // 2
            for r in halves:
                for u in range(2):
                    nc.tensor.transpose(
                        bank[:, P * (2 * r + u) : P * (2 * r + u + 1)],
                        pairs[:, per_half * r + u : per_half * (r + 1) : 2],
                        ident[:],
                    )

        def turn_x(i, bank_name):
            tiles["xT", i] = psum.tile([P, BANK], F32, name=bank_name)
            turn(tiles["x", i], tiles["xT", i], range(HALVES))

        def copy_x(i):
            tiles["xg", i] = work.tile([P, PACK * UNIT], BF16, name="x_grouped", align_bytes=64)
            nc.scalar.copy(
                out=tiles["xg", i][:].bitcast(F32).rearrange("k (r p u) -> k r p u", r=HALVES, u=2),
                in_=tiles["xT", i][:].rearrange("k (r u p) -> k r p u", r=HALVES, u=2),
            )

        def quantize_x(i):
            tiles["xq", i] = work.tile([P, UNIT], U32, name="x_codes", bufs=3, align_bytes=64)
            tiles["xs", i] = work.tile([P, UNIT], U8, name="x_scales", bufs=3, align_bytes=64)
            nc.vector.quantize_mx(
                out=tiles["xq", i][:].bitcast(FP8X4), scales=tiles["xs", i][:], in_=tiles["xg", i][:]
            )


        def first_product(n):
            if n >= S_TILES * UNITS:
                return
            i, (h, r) = n // S_TILES, divmod(n % S_TILES, HALVES)
            g = i // PER_GROUP
            samples = slice(P * r, P * (r + 1))
            tiles["S", n] = psum.tile([P, BANK], F32, name="s_bank", bufs=S_BANKS)
            for t in range(PACK):
                slot = PACK * h + t
                nc.tensor.matmul_mx(
                    out=tiles["S", n][:, P * t : P * (t + 1)],
                    lhsT=tiles["c", g][:, FP4_WORD * P * slot : FP4_WORD * P * (slot + 1)].bitcast(FP4X4),
                    lhsT_scale=tiles["c_plane", g][:, P * slot : P * (slot + 1)],
                    rhs=tiles["xq", i][:, samples].bitcast(FP8X4),
                    rhs_scale=tiles["xs", i][:, samples],
                    start=True,
                    stop=True,
                )

        def exponential(n):
            if n >= S_TILES * UNITS:
                return
            i, (h, r) = n // S_TILES, divmod(n % S_TILES, HALVES)
            if r == 0:
                tiles["E", i, h] = work.tile([P, PACK * UNIT], F32, name="exp_s", bufs=4)
            nc.scalar.activation(
                out=tiles["E", i, h][:, BANK * r : BANK * (r + 1)].rearrange("p (n t) -> p n t", t=PACK),
                in_=tiles["S", n][:].rearrange("p (t n) -> p n t", t=PACK),
                func=ACT.Exp,
            )

        def times_rulefac(i, h):
            row = RULE_PASSES * (i // PER_GROUP) + h
            if h == 0:
                tiles["H", i] = work.tile([P, RULE_PASSES * PACK * UNIT], BF16, name="h_grouped", align_bytes=64)
            nc.vector.tensor_tensor(
                out=tiles["H", i][:, PACK * UNIT * h : PACK * UNIT * (h + 1)].rearrange("p (n t) -> p n t", t=PACK),
                in0=tiles["E", i, h][:].rearrange("p (n t) -> p n t", t=PACK),
                in1=rule_quads[:, PACK * row : PACK * (row + 1)].unsqueeze(1).to_broadcast([P, UNIT, PACK]),
                op=ALU.mult,
            )

        def quantize_h(i):
            tiles["hq", i] = work.tile([P, RULE_PASSES * UNIT], U32, name="h_codes", bufs=3, align_bytes=64)
            tiles["hs", i] = work.tile([P, RULE_PASSES * UNIT], U8, name="h_scales", bufs=3, align_bytes=64)
            nc.vector.quantize_mx(
                out=tiles["hq", i][:].bitcast(FP8X4), scales=tiles["hs", i][:], in_=tiles["H", i][:]
            )


        def second_product(i, r, bank_name, banks):
            g = i // PER_GROUP
            tiles["U", i, r] = psum.tile([P, BANK], F32, name=bank_name, bufs=banks)
            for h in range(RULE_PASSES):
                samples = slice(UNIT * h + P * r, UNIT * h + P * (r + 1))
                f_pass = RULE_PASSES * g + h
                nc.tensor.matmul_mx(
                    out=tiles["U", i, r][:],
                    lhsT=tiles["hq", i][:, samples].bitcast(FP8X4),
                    lhsT_scale=tiles["hs", i][:, samples],
                    rhs=tiles["f", g][:, FP4_WORD * M * h : FP4_WORD * M * (h + 1)].bitcast(FP4X4),
                    rhs_scale=f_plane[:, M * f_pass : M * (f_pass + 1)],
                    start=(h == 0),
                    stop=(h == RULE_PASSES - 1),
                )

        def times_err(i, r):
            if r == 0:
                tiles["V", i] = work.tile([P, HALVES * M], F32, name="gain_err", bufs=3)
                tiles["y", i] = work.tile([P, HALVES * M], F32, name="y_sb", bufs=4)
                tiles["yb", i] = work.tile([P, HALVES * M], BF16, name="y_bf16", bufs=3)
            nc.vector.scalar_tensor_tensor(
                out=tiles["V", i][:, half_cols(r, 1)],
                in0=tiles["err", i][:, half_cols(r, 1)],
                scalar=row_f32[:, HALVES * i + r : HALVES * i + r + 1],
                in1=tiles["U", i, r][:],
                op0=ALU.mult,
                op1=ALU.mult,
            )

        def add_u0_and_store(engine, i, first, count):
            cols = half_cols(first, count)
            engine.tensor_tensor(
                out=tiles["y", i][:, cols].rearrange("p (r j) -> p r j", r=count),
                in0=tiles["V", i][:, cols].rearrange("p (r j) -> p r j", r=count),
                in1=tiles["u0", i // PER_GROUP][:].unsqueeze(1).to_broadcast([P, count, M]),
                op=ALU.add,
            )
            nc.sync.dma_start(out=unit_rows(y_rows, i)[:, cols], in_=tiles["y", i][:, cols])

        def round_y(copy, i, first, count):
            cols = half_cols(first, count)
            copy(out=tiles["yb", i][:, cols], in_=tiles["y", i][:, cols])

        def turn_y(i, bank_name, halves):
            tiles["yT", i] = psum.tile([P, BANK], F32, name=bank_name)
            turn(tiles["yb", i], tiles["yT", i], halves)

        def copy_y(i):
            tiles["yg", i] = work.tile([P, PACK * UNIT], BF16, name="y_grouped", bufs=3, align_bytes=64)
            nc.scalar.copy(
                out=tiles["yg", i][:].bitcast(F32).rearrange("k (p r u) -> k p r u", r=HALVES, u=2),
                in_=tiles["yT", i][:].rearrange("k (r u p) -> k p r u", r=HALVES, u=2),
            )

        def quantize_y(i):
            g, j = divmod(i, PER_GROUP)
            pair, place = divmod(i, 2)
            if place == 0:
                tiles["yq", pair] = work.tile([P, 2 * UNIT], U32, name="y_codes", bufs=3, align_bytes=64)
            if j == 0:
                tiles["ys", g] = work.tile([P, N], U8, name="y_scales", align_bytes=64)
            codes = tiles["yq", pair]
            own = slice(UNIT * place, UNIT * (place + 1))
            nc.vector.quantize_mx(
                out=codes[:, own].bitcast(FP8X4),
                scales=tiles["ys", g][:, UNIT * j : UNIT * (j + 1)],
                in_=tiles["yg", i][:],
            )
            if i >= UNITS - 2:
                nc.sync.dma_start(out=out_words[:, UNIT * i : UNIT * (i + 1)], in_=codes[:, own].bitcast(I32))
            elif place == 1:
                nc.sync.dma_start(out=out_words[:, UNIT * (i - 1) : UNIT * (i + 1)], in_=codes[:].bitcast(I32))
            if j == PER_GROUP - 1:
                for q in range(QUADRANTS):
                    queue = nc.scalar if g == G - 1 and q % 2 == 1 else nc.sync
                    queue.dma_start(
                        out=out_2[0, 4 * q : 4 * q + 4, N * g : N * (g + 1)].bitcast(I32),
                        in_=tiles["ys", g][32 * q : 32 * q + 4, :].bitcast(I32),
                    )

        ident = keep.tile([P, P], F32)
        c_scale_rows = keep.tile([P, R], U8)
        c_plane_first = keep.tile([P, R], U8, align_bytes=64)
        c_plane_rest = keep.tile([P, (G - 1) * R], U8, align_bytes=64)
        f_plane = keep.tile([P, G * RULE_PASSES * M], U8, align_bytes=64)
        rule_rows = keep.tile([P, K_PASS], BF16)
        row_bf16 = keep.tile([P, HALVES * UNITS], BF16)
        row_f32 = keep.tile([P, HALVES * UNITS], F32)

        nc.vector.memset(c_scale_rows[:].bitcast(I32), 0)
        nc.vector.memset(rule_rows[:], 0.0)
        make_identity(nc, ident[:])
        nc.vector.memset(c_plane_rest[:].bitcast(I32), 0)
        nc.vector.memset(f_plane[:].bitcast(I32), 0)

        tiles["c_plane", 0] = c_plane_first[:]
        for g in range(1, G):
            tiles["c_plane", g] = c_plane_rest[:, R * (g - 1) : R * g]

        load_x(0)
        load_c_words(0)
        for q in range(QUADRANTS):
            nc.sync.dma_start(
                out=c_scale_rows[32 * q : 32 * q + 4 * G, :].bitcast(I32),
                in_=c_scales[:, 4 * q : 4 * q + 4, :].bitcast(I32),
            )
        load_x(1)
        nc.sync.dma_start(
            out=rule_rows[0 : G * RULE_PASSES, :], in_=rulefac.rearrange("g (h k) -> (g h) k", h=RULE_PASSES)
        )
        load_x(2)
        load_c_words(1)
        load_c_words(2)
        load_f_words(0)
        for q in range(QUADRANTS):
            nc.sync.dma_start(
                out=f_plane[32 * q : 32 * q + 4, :].bitcast(I32).rearrange("s (c n) -> s c n", c=G * RULE_PASSES),
                in_=f_scales[:, 4 * q : 4 * q + 4, :].rearrange("c s n -> s c n").bitcast(I32),
            )
        load_x(3)
        nc.sync.dma_start(
            out=row_bf16[:].rearrange("p (i r) -> p i r", r=HALVES),
            in_=rowfac.rearrange("g (j p r) -> p (g j) r", p=P, r=HALVES),
        )
        load_u0(0)
        load_err(0)

        turn_x(0, "x_bank")
        turn_x(1, "y_bank")
        load_x(4)
        rule_bank = psum.tile([P, BANK], F32)
        rule_pairs = rule_rows[:].bitcast(F32)
        for u in range(2):
            nc.tensor.transpose(rule_bank[:, u : 2 * P : 2], rule_pairs[:, u : K_PASS // 2 : 2], ident[:])
        rule_quads = rule_bank[:].bitcast(BF16)
        nc.gpsimd.tensor_copy(out=row_f32[:], in_=row_bf16[:])
        sort_c_words(0, 0)
        sort_c_scales()
        copy_x(0)
        quantize_x(0)
        sort_c_words(0, 1)
        copy_x(1)
        for n in range(S_BANKS):
            first_product(n)
        quantize_x(1)
        for h in range(RULE_PASSES):
            sort_c_words(1, h)
        sort_c_words(2, 0)
        for n in range(S_TILES):
            exponential(n)
            first_product(n + S_BANKS)
            if n == 1:
                turn_x(2, "x_bank")
                times_rulefac(0, 0)
                sort_c_words(2, 1)

        for s in range(UNITS):
            g, j = divmod(s, PER_GROUP)
            n = S_TILES * (s + 1)
            if live(s + X_AHEAD):
                load_x(s + X_AHEAD)
            if live(s + 1):
                load_err(s + 1)
            if s == 0:
                load_c_words(G - 1)
            if j == 0 and g + 1 < G:
                spread_c_scales(g + 1)
            if j == 1 and g + 1 < G:
                load_f_words(g + 1)
                load_u0(g + 1)

            if live(s - 1):
                second_product(s - 1, 0, "u_bank", U_BANKS)
            if live(s - 2):
                times_err(s - 2, 1)
                add_u0_and_store(nc.gpsimd, s - 2, 0, HALVES)
            if live(s - 3):
                round_y(nc.scalar.copy, s - 3, 0, HALVES)
            if live(s + 2):
                copy_x(s + 2)
            if live(s - 3):
                turn_y(s - 3, "y_bank", range(HALVES))
            if live(s + 3):
                turn_x(s + 3, "x_bank")
            if live(s - 1):
                second_product(s - 1, 1, "u_bank", U_BANKS)
            for h in range(1 if s == 0 else 0, RULE_PASSES):
                times_rulefac(s, h)
            if live(s - 1):
                times_err(s - 1, 0)
            exponential(n)
            first_product(n + S_BANKS)
            exponential(n + 1)
            if live(s - 3):
                copy_y(s - 3)
            if live(s + 2):
                quantize_x(s + 2)
            if g == 1 and j < RULE_PASSES:
                sort_c_words(G - 1, j)
            quantize_h(s)
            if live(s - 4):
                quantize_y(s - 4)
            first_product(n + 1 + S_BANKS)
            for later in (n + 2, n + 3):
                exponential(later)
                first_product(later + S_BANKS)

        third_last, second_last, last = UNITS - 3, UNITS - 2, UNITS - 1
        second_product(last, 0, "u_bank", U_BANKS)
        second_product(last, 1, "s_bank", S_BANKS)
        times_err(second_last, 1)
        add_u0_and_store(nc.gpsimd, second_last, 1, 1)
        round_y(nc.scalar.copy, third_last, 0, HALVES)
        turn_y(third_last, "y_bank", range(HALVES))
        for r in range(HALVES):
            times_err(last, r)
        copy_y(third_last)
        for i, r in ((second_last, 0), (last, 0), (last, 1)):
            add_u0_and_store(nc.vector, i, r, 1)
        for r in (1, 0):
            round_y(nc.scalar.copy, second_last, r, 1)
        turn_y(second_last, "y_bank", (1, 0))
        for r in range(HALVES):
            round_y(nc.vector.tensor_copy, last, r, 1)
        turn_y(last, "x_bank", range(HALVES))
        for i in (third_last - 1, third_last):
            quantize_y(i)
        for i in (second_last, last):
            copy_y(i)
            quantize_y(i)
